import numpy as np, ml_dtypes
CORES = [16,18,20,22]
N = 4
BF = ml_dtypes.bfloat16
def gentries(a):
    return np.ascontiguousarray(a.reshape(8, 16, -1).transpose(0, 2, 1)).reshape(8, -1)
def gtable(e):
    e = np.asarray(e); return np.ascontiguousarray(e.reshape(8, -1, 16).transpose(0, 2, 1)).reshape(128, -1).astype(np.int32)
R, F, C, D, B = 8192, 4096, 1536, 2, 1 << 20
def passing(at, lim):
    a0 = at[:, 0].reshape(8, R); l = lim.reshape(8, 2)
    return (a0 >= l[:, :1]) & (a0 <= l[:, 1:])
def dims(rng, m, w, first=None):
    lo = rng.integers(-(B >> 1), B >> 2, (8, 1)); hi = lo + w[:, None]; z = rng.random((8, R))
    if first is not None: z[np.arange(8), first] = -1
    ok = np.argsort(np.argsort(z, 1), 1) < m[:, None]
    out = np.where(rng.random((8, R)) < 0.5, rng.integers(1 - B, lo, (8, R)), rng.integers(hi + 1, B, (8, R)))
    return lo, hi, ok, np.where(ok, rng.integers(lo, hi + 1, (8, R)), out)
def living(n, z):
    return np.argsort(np.argsort(z, 1), 1) < n[:, None]
def facts(rng, ok, live, p, where, e=1):
    m = np.sum(ok, axis=1)[:, None]; o = np.argsort(~ok, 1, kind="stable")
    bad = rng.random((N, 8, F)) < p; np.put_along_axis(bad, where, True, 1); bad = bad & ~live[:, None]
    k = np.where(bad, R - m, m); j = np.minimum((rng.random((N, 8, F)) ** e * k).astype(np.int64), k - 1)
    return o[np.arange(8)[:, None], j + np.where(bad, m, 0)]
def pack(lo, hi, v, rest, fk, me):
    rest[:, 0] = v
    return {"at": np.ascontiguousarray(rest.reshape(N, D, 16, R).transpose(0, 2, 1, 3)).reshape(N, 16, D * R).astype(np.int32),
            "lim": np.concatenate([lo, hi], 1).reshape(N, 1, 2 * D).astype(np.int32), "fk": np.stack([gtable(x) for x in fk]), "me": me.reshape(N, 1, F).astype(np.int32)}
def whole(rng, *shape):
    return rng.integers(1 - B, B, shape)
def setup_inputs(rng):
    lo, hi, ok, v = dims(rng, rng.integers(R // 4, 3 * R // 4, 8), rng.integers(B >> 6, B >> 2, 8))
    live = living(rng.integers(C // 4, C, N), rng.random((N, F)))
    return pack(lo, hi, v, whole(rng, 8, 16, R), facts(rng, ok, live, 0.15, rng.integers(0, 8, (N, 1, F))), whole(rng, N, F))
def setup_inputs_full(rng):
    lo, hi, ok, v = dims(rng, rng.integers(R // 4, 3 * R // 4, 8), rng.integers(B >> 6, B >> 2, 8))
    n = np.full(N, C); n[rng.integers(0, N)] = 1; z = rng.random((N, F)); z[:, 0] = -1; z[:, -1] = -2
    return pack(lo, hi, v, whole(rng, 8, 16, R), facts(rng, ok, living(n, z), 0.3, rng.integers(0, 8, (N, 1, F))), whole(rng, N, F))
def setup_inputs_ends(rng):
    w = np.where(rng.permutation(8) < 3, 0, rng.integers(1, 1000, 8))
    lo, hi, ok, v = dims(rng, rng.integers(R // 4, 3 * R // 4, 8), w); h = rng.random((8, R)) < 0.5
    v = np.where(ok, np.where(h, lo, hi), np.where(h, lo - 1, hi + 1)); j = np.arange(F)
    live = living(rng.integers(C // 4, C + 1, N), np.minimum(j, F - 1 - j)[None] + np.zeros((N, 1)))
    return pack(lo, hi, v, whole(rng, 8, 16, R), facts(rng, ok, live, 0.1, rng.integers(0, 8, (N, 1, F))), whole(rng, N, F))
def setup_inputs_alike(rng):
    m = np.where(rng.permutation(8) < 4, 1, R - 1)
    lo, hi, ok, v = dims(rng, m, rng.integers(0, B >> 2, 8), np.where(rng.random(8) < 0.5, 0, R - 1))
    live = living(rng.integers(C // 4, C + 1, N), rng.random((N, F))); fk = facts(rng, ok, live, 0.1, rng.integers(0, 8, (N, 1, F)))
    q = rng.integers(0, N); s = np.flatnonzero(live[q]); fk[q][:, s] = fk[q][:, s[:1]]
    return pack(lo, hi, v, whole(rng, 8, 16, R), fk, whole(rng, N, F))
def setup_inputs_near(rng):
    lo, hi, ok, v = dims(rng, rng.integers(R // 4, 3 * R // 4, 8), rng.integers(B >> 6, B >> 2, 8))
    where = np.where(rng.random((N, 1, 1)) < 0.5, rng.integers(0, 8, (N, 1, 1)), rng.integers(0, 8, (N, 1, F)))
    live = living(rng.integers(C // 4, C + 1, N), rng.random((N, F))); sg = rng.choice(np.array([-1, 1]), (1, 16, 1))
    rest = sg * (B - 1 - rng.integers(0, 50, (8, 16, R))); me = rng.choice(np.array([-1, 1]), (N, 1)) * (B - 1 - rng.integers(0, 50, (N, F)))
    return pack(lo, hi, v, rest, facts(rng, ok, live, 0.0, where), me)
def setup_inputs_spread(rng):
    lo, hi, ok, v = dims(rng, np.maximum(1, R >> rng.integers(1, 10, 8)), 1 << rng.integers(0, 18, 8))
    live = living(np.maximum(1, C >> rng.integers(0, 6, N)), rng.random((N, F)))
    rest = whole(rng, 8, 16, R) >> rng.integers(0, 20, (8, 16, R)); me = whole(rng, N, F) >> rng.integers(0, 20, (N, F))
    return pack(lo, hi, v, rest, facts(rng, ok, live, rng.random((1, 8, 1)), rng.integers(0, 8, (N, 1, F)), 4), me)
def check_inputs(d):
    bad = [k for k in ("at", "lim", "me") if not ((d[k] > -B) & (d[k] < B)).all()]
    if not ((d["fk"] >= 0) & (d["fk"] < R)).all(): return bad + ["fk"]
    ok = passing(d["at"], d["lim"]); g = np.arange(8)[:, None]
    n = [int(np.sum(np.all(ok[g, gentries(a)], axis=0))) for a in d["fk"]]
    return bad + ([] if min(n) >= 1 and max(n) <= C else ["survivors"])
def reference(at, lim, fk, me):
    y = np.zeros((N, 16, C + 1), np.int64); ok = passing(at, lim); g = np.arange(8)[:, None]
    a = np.ascontiguousarray(at.reshape(N, 16, D, R).transpose(0, 2, 1, 3)).reshape(8, 16, R).astype(np.int64)
    for r in range(N):
        k = gentries(fk[r]); s = np.flatnonzero(np.all(ok[g, k], axis=0)); n = len(s)
        y[r, :, :n] = me[r, 0][s][None]
        for d in range(8): y[r, :, :n] += a[d][:, k[d, s]]
        y[r, :, C] = n
    return {"y": np.asarray(y, np.float32)}

@@ -1,0 +1,355 @@
+from concourse.bass import DstId, RemoteDMATransfer
+from concourse.mybir import AluOpType as A, ActivationFunctionType as AF
+import numpy as np
+
+R, F, C, D, NR = 8192, 4096, 1536, 2, 4
+TR = 3584
+EARLY = 2
+P1, P2 = 2560, 4608
+
+SCRATCH = {
+    "limi": ("sbuf", [128, 2], "int32"), "limf": ("sbuf", [128, 2], "float32"),
+    "a0": ("sbuf", [128, 128], "int32"), "ps": ("sbuf", [128, 128], "bfloat16"),
+    "PD": ("dram", [NR, 128, 128], "bfloat16"),
+    "pw": ("sbuf", [128, R], "bfloat16"), "Pg": ("sbuf", [128, F], "bfloat16"),
+    "fkt": ("sbuf", [128, 256], "int32"), "off16": ("sbuf", [128, 256], "uint16"),
+    "fhi": ("sbuf", [128, 256], "int32"), "flo": ("sbuf", [128, 256], "int32"),
+    "fhib": ("sbuf", [128, 256], "bfloat16"), "flob": ("sbuf", [128, 256], "bfloat16"),
+    "K1": ("sbuf", [128, 512], "bfloat16"), "W1": ("sbuf", [128, TR], "bfloat16"),
+    "mei": ("sbuf", [128, 32], "int32"), "mep": ("sbuf", [128, 96], "int32"),
+    "MEL": ("sbuf", [128, 512], "bfloat16"), "MeR": ("sbuf", [128, 512], "bfloat16"),
+    "Wm": ("sbuf", [128, TR], "bfloat16"),
+    "onesb": ("sbuf", [128, 128], "bfloat16"), "onesf": ("sbuf", [128, 128], "float32"),
+    "zb": ("sbuf", [128, 128], "bfloat16"),
+    "limsel": ("sbuf", [128, 128], "float32"), "Qt": ("sbuf", [128, 260], "bfloat16"),
+    "YY": ("sbuf", [128, 144], "bfloat16"), "kc": ("sbuf", [128, 1], "int32"),
+    "kx": ("sbuf", [128, 1], "int32"), "kxf": ("sbuf", [128, 1], "float32"),
+    "ku": ("sbuf", [128, 1], "int32"), "kuf": ("sbuf", [128, 1], "float32"),
+    "row2d": ("sbuf", [128, 8], "float32"), "rowj": ("sbuf", [128, 32], "float32"),
+    "J": ("sbuf", [128, 32], "float16"),
+    "mats": ("sbuf", [128, 384], "bfloat16"), "H": ("sbuf", [128, 640], "float16"),
+    "idb": ("sbuf", [128, 128], "bfloat16"), "idf": ("sbuf", [128, 128], "float32"),
+    "sele": ("sbuf", [128, 64], "float32"),
+    "Msk": ("sbuf", [128, 32], "float16"), "Sc": ("sbuf", [128, 16], "float16"),
+    "MJ": ("sbuf", [128, 32], "float16"), "off3": ("sbuf", [128, 32], "uint16"),
+    "nt": ("sbuf", [128, 1], "float32"),
+    "Lu": ("sbuf", [128, 96], "uint16"), "Lr": ("sbuf", [128, NR * 96], "uint16"),
+    "off2": ("sbuf", [128, 96], "uint16"),
+    "ATW": ("sbuf", [128, R + 8], "int32"), "G": ("sbuf", [128, C], "float32"),
+    "SA": ("sbuf", [128, 512], "float32"), "LA": ("sbuf", [128, 512], "float32"),
+    "SB0": ("sbuf", [128, 128], "float32"), "LB0": ("sbuf", [128, 128], "float32"),
+    "SB1": ("sbuf", [128, 128], "float32"), "LB1": ("sbuf", [128, 128], "float32"),
+    "accA": ("sbuf", [128, 128], "float32"), "tB": ("sbuf", [128, 64], "float32"),
+    "OA": ("sbuf", [128, 128], "float32"), "OB": ("sbuf", [128, 64], "float32"),
+}
+for _b in range(8):
+    SCRATCH["b%d" % _b] = ("psum", [128, 512], "float32")
+NEV = 122
+SEMAPHORES = (["e%d" % _i for _i in range(NEV)] + ["left", "h1"]
+              + ["%s_%d" % (_n, _q) for _n in ("h2", "h3a", "h3b0", "h3b1") for _q in range(NR)])
+
+
+def rank_program(g, core, T, topo):
+    q = T.rank_of(core)
+    if q is None:
+        return
+    V, S, PE, SY = g.vector, g.scalar, g.tensor, g.sync
+    queues = {"g": g, "v": V, "s": S, "p": PE, "y": SY}
+    used, total, seen, waited = [0], {}, {}, {}
+
+    def new():
+        s = "e%d" % used[0]
+        used[0] += 1
+        return s
+
+    def ev(inst, n=1, s=None):
+        if s is None:
+            s = new()
+        inst.then_inc(T.sem[s], n)
+        total[s] = total.get(s, 0) + n
+        return s
+
+    def wait(k, *names):
+        for s in names:
+            n = total[s]
+            if seen.get((k, s), 0) < n:
+                queues[k].wait_ge(T.sem[s], n)
+                seen[(k, s)] = n
+                waited[s] = max(waited.get(s, 0), n)
+
+    others = [c for c in T.cores if c != core]
+    cross = [c for c in others if topo.die(c) != topo.die(core)]
+    same = [c for c in others if topo.die(c) == topo.die(core)]
+    dests = cross[:1] + same + cross[1:]
+    order = [T.rank_of(c) for c in dests]
+    total["h1"] = 12
+    for n in ("h2", "h3a", "h3b0", "h3b1"):
+        for r in order:
+            total["%s_%d" % (n, r)] = 4
+
+    def send(rsem, src, dst):
+        tr = []
+        for k, c in enumerate(dests):
+            rid, pid, _ = topo.addr(c)
+            mask = sum(1 << e for e in topo.engines(core, c)[k::4])
+            tr.append(RemoteDMATransfer(dst_ids=[DstId(rid=rid, pnc=pid)], dma_engine_mask=mask,
+                                        remote_sem=T.sem[rsem], src=src(T.rank_of(c)), dst=dst))
+        g.remote_dma_fused(tr, local_sem=T.sem.left)
+        total["left"] = total.get("left", 0) + 4 * len(dests)
+
+    def at_load(k):
+        r, e = k // 2, k % 2
+        p = 32 * r + 16 * e
+        return SY.dma_start(T.ATW[p:p + 16, 0:R], T.at[:, R * e:R * e + R])
+
+    d_lim = ev(SY.dma_start(T.limi[0:2, :], T.lim[0:1, :]), 16)
+    d_a0 = ev(S.dma_start(T.a0[:, :], T.at[0:1, :]), 16)
+    d_fk = ev(S.dma_start(T.fkt[:, :], T.fk[:, :]), 16)
+    d_me = ev(SY.dma_start(T.mei[:, 0:16], T.me[0:1, 0:2048]), 16)
+    ev(SY.dma_start(T.mei[:, 16:32], T.me[0:1, 2048:4096]), 16, d_me)
+    d_at = new()
+    for k in range(EARLY):
+        ev(at_load(k), 16, d_at)
+
+    z0 = ev(V.memset(T.pw[:, 0:1024], 0.0))
+    m_one = ev(V.memset(T.onesf[:, :], 1.0))
+    ev(V.memset(T.onesb[:, :], 1.0), 1, m_one)
+    m_z = ev(V.memset(T.zb[:, :], 0.0))
+    ev(V.memset(T.Qt[:, :], 0.0), 1, m_z)
+    z1 = ev(V.memset(T.pw[:, 1024:P1], 0.0))
+    wait("s", z0)
+    z2 = new()
+    for k in range(P2, R, 1024):
+        n = min(1024, R - k)
+        ev(S.activation(T.pw[:, k:k + n], T.pw[:, 0:n], AF.Copy), 1, z2)
+
+    wait("g", m_one)
+    c_lim = ev(g.affine_select(T.limsel[0:2, :], T.onesf[0:2, :], [[1, 2], [0, 64]], A.is_equal, 0.0, 0, -1))
+    wait("g", m_z)
+    c_q = new()
+    for h in range(2):
+        ev(g.affine_select(T.Qt[:, 130 * h + 1:130 * h + 129:2], T.onesb[:, 0:64], [[2, 8], [16, 8]],
+                           A.is_equal, 0.0, h, -1), 1, c_q)
+    c_io = ev(g.iota(T.kc[:, :], [[0, 1]], 0, 1))
+    ev(g.iota(T.row2d[:, :], [[2, 8]], 0, 0, allow_small_or_imprecise_dtypes=True), 1, c_io)
+    ev(g.iota(T.rowj[:, :], [[1, 2], [32, 16]], C, 0, allow_small_or_imprecise_dtypes=True), 1, c_io)
+
+    wait("v", d_lim)
+    v_lim = ev(V.tensor_copy(T.limf[0:2, :], T.limi[0:2, :]))
+    wait("p", v_lim, c_lim)
+    p_lim = ev(PE.matmul(T.b2[:, 480:482], T.limsel[0:2, :], T.limf[0:2, :], True, True))
+    wait("v", d_a0, p_lim)
+    v_cl = ev(V.tensor_scalar(out=T.b2[:, 128:256], in0=T.a0[:, :], scalar1=T.b2[:, 480:481],
+                              scalar2=T.b2[:, 481:482], op0=A.max, op1=A.min))
+    wait("v", v_cl)
+    v_ps = ev(V.tensor_tensor(T.ps[:, :], T.b2[:, 128:256], T.a0[:, :], A.is_equal))
+    wait("g", v_ps)
+    send("h1", lambda r: T.ps[:, :], T.PD[q])
+    ev(V.memset(T.pw[:, P1:P2], 0.0), 1, z1)
+    wait("y", v_ps, z0, z1, z2)
+    d_pw = ev(SY.dma_start(T.pw[32 * q:32 * q + 32:16, :], T.ps[:, :]), 16)
+    wait("y", "h1")
+    for lo, hi in ((0, q), (q + 1, NR)):
+        if lo < hi:
+            ev(SY.dma_start(T.pw[32 * lo:32 * hi:16, :], T.PD[lo:hi]), 16, d_pw)
+    for k in range(EARLY, 8):
+        ev(at_load(k), 16, d_at)
+
+    wait("v", d_fk)
+    v_off = ev(V.tensor_copy(T.off16[:, :], T.fkt[:, :]))
+    v_k = ev(V.tensor_scalar(out=T.fhi[:, :], in0=T.fkt[:, :], scalar1=0x1F80, scalar2=None, op0=A.bitwise_and))
+    ev(V.tensor_scalar(out=T.flo[:, :], in0=T.fkt[:, :], scalar1=127, scalar2=None, op0=A.bitwise_and), 1, v_k)
+    wait("v", v_k)
+    v_kb = ev(V.tensor_scalar(out=T.fhib[:, :], in0=T.fhi[:, :], scalar1=-8192.0, scalar2=None, op0=A.add))
+    ev(V.tensor_copy(T.flob[:, :], T.flo[:, :]), 1, v_kb)
+    wait("p", v_kb, c_q)
+    p_r = new()
+    for h in range(2):
+        o = T.b0[:, 256 * h:256 * h + 256]
+        ev(PE.matmul(o, T.Qt[:, 130 * h + 1:130 * h + 129], T.fhib[:, :], True, False), 1, p_r)
+        ev(PE.matmul(o, T.Qt[:, 130 * h:130 * h + 128], T.flob[:, :], False, True), 1, p_r)
+    wait("s", p_r)
+    s_k1 = ev(S.activation(T.K1[:, :], T.b0[:, :], AF.Copy))
+
+    c_idb = ev(g.affine_select(T.idb[:, :], T.onesb[:, :], [[1, 128]], A.is_equal, 0.0, 0, -1))
+    c_m = new()
+    pat = [[1, 8], [8, 16]]
+    ev(g.affine_select(T.mats[:, 0:128], T.zb[:, :], pat, A.is_gt, -1.0, 0, -1), 1, c_m)
+    ev(g.affine_select(T.mats[:, 128:256], T.zb[:, :], pat, A.is_ge, -1.0, 0, -1), 1, c_m)
+    ev(g.affine_select(T.mats[:, 256:384], T.onesb[:, :], pat, A.is_equal, 0.0, 0, -1), 1, c_m)
+    z_w1 = ev(g.iota(T.W1[:, 0:C], [[0, C]], 0, 0, allow_small_or_imprecise_dtypes=True))
+    c_s1 = ev(g.affine_select(T.sele[:, :], T.onesf[:, 0:64], [[32, 4], [1, 16]], A.is_equal, 0.0, 0, -1))
+    c_idf = ev(g.affine_select(T.idf[:, :], T.onesf[:, :], [[1, 128]], A.is_equal, 0.0, 0, -1))
+    wait("g", c_s1)
+    c_sel = ev(g.affine_select(T.sele[:, :], T.sele[:, :], [[32, 4], [1, 16]], A.not_equal, 1.0, 16, -1))
+
+    m_w = ev(V.memset(T.ATW[:, R:R + 8], 0))
+    m_mel = ev(V.memset(T.MEL[:, :], 0.0))
+    wait("v", d_me, c_io)
+    v_mp = ev(V.tensor_scalar(out=T.mep[:, 0:32], in0=T.mei[:, :], scalar1=14, scalar2=None, op0=A.arith_shift_right))
+    ev(V.tensor_scalar(out=T.mep[:, 32:64], in0=T.mei[:, :], scalar1=0x3F80, scalar2=None, op0=A.bitwise_and), 1, v_mp)
+    ev(V.tensor_scalar(out=T.mep[:, 64:96], in0=T.mei[:, :], scalar1=127, scalar2=None, op0=A.bitwise_and), 1, v_mp)
+    v_ku = ev(V.tensor_scalar(out=T.ku[:, :], in0=T.kc[:, :], scalar1=3, scalar2=None, op0=A.arith_shift_right))
+    v_kx = ev(V.tensor_scalar(out=T.kx[:, :], in0=T.kc[:, :], scalar1=14, scalar2=None, op0=A.bitwise_and))
+    wait("v", v_mp, m_mel)
+    v_mel = new()
+    for x in range(3):
+        for h in range(2):
+            ev(V.tensor_scalar(out=T.MEL[:, 256 * h + x:256 * h + 256:16], in0=T.mep[:, 32 * x + h:32 * x + 32:2],
+                               scalar1=16384.0 if x == 0 else 1.0, scalar2=None, op0=A.mult), 1, v_mel)
+    wait("v", v_ku)
+    v_kf = ev(V.tensor_scalar(out=T.kuf[:, :], in0=T.ku[:, :], scalar1=2.0, scalar2=None, op0=A.mult))
+    wait("p", v_mel, c_idb)
+    p_me = new()
+    for x in range(4):
+        ev(PE.matmul(T.b1[:, 128 * x:128 * x + 128], T.MEL[:, 128 * x:128 * x + 128], T.idb[:, :], True, True), 1, p_me)
+
+    wait("v", d_pw, v_off, z0, z1)
+    wait("s", d_pw, v_off, z0, z1)
+    p_c = new()
+    vgot = []
+    for lo, hi in ((0, 3), (3, 5), (5, 7), (7, 8)):
+        got = [ev(V.tensor_copy(T.Pg[:, 256 * lo:256 * hi], T.pw[:, :].indirect(T.off16[:, 16 * lo:16 * hi]))),
+               ev(S.activation(T.Pg[:, 2048 + 256 * lo:2048 + 256 * hi],
+                               T.pw[:, :].indirect(T.off16[:, 128 + 16 * lo:128 + 16 * hi]), AF.Copy))]
+        vgot.append(got[0])
+        for b in range(2):
+            wait("p", got[b])
+            for uh in range(8 * b + lo, 8 * b + hi):
+                for h in range(2):
+                    w = 16 * h + uh
+                    ev(PE.matmul(T.b2[:, w:w + 1], T.Pg[:, 256 * uh + h:256 * uh + 256:2], T.onesb[:, 0:1], True, True),
+                       1, p_c)
+    wait("s", p_me)
+    s_mer = ev(S.activation(T.MeR[:, :], T.b1[:, :], AF.Copy))
+    wait("s", *vgot)
+    z_wm = ev(S.activation(T.Wm[:, 0:C], T.Pg[:, 0:C], AF.Copy, scale=0.0))
+
+    wait("v", c_m, v_kf)
+    v_h = ev(V.tensor_copy(T.H[:, 0:384], T.mats[:, :]))
+    v_j = ev(V.tensor_scalar(out=T.J[:, :], in0=T.rowj[:, :], scalar1=T.kuf[:, :], scalar2=None, op0=A.add))
+    ev(V.tensor_copy(T.H[:, 512:640], T.onesb[:, :]), 1, v_h)
+    ev(V.tensor_scalar(out=T.H[:, 384:512], in0=T.mats[:, 256:384], scalar1=-1.0, scalar2=None, op0=A.mult), 1, v_h)
+    L1, L1B, IP, NIP, ONE = [T.H[:, 128 * k:128 * k + 128] for k in range(5)]
+    wait("p", v_h, v_j)
+    PE.matmul(T.b3[:, 0:32], IP, T.J[:, :], True, False)
+    wait("v", p_c)
+    v_m = ev(V.tensor_scalar(out=T.Msk[:, :], in0=T.b2[:, 0:32], scalar1=7.5, scalar2=None, op0=A.is_gt))
+    wait("v", v_m)
+    v_sc = ev(V.tensor_tensor_scan(T.Sc[:, :], T.Msk[:, 0:16], T.Msk[:, 16:32], 0.0, A.add, A.add))
+    v_mj = ev(V.tensor_tensor(T.MJ[:, :], T.Msk[:, :], T.J[:, :], A.mult))
+    wait("p", v_m)
+    PE.matmul(T.b3[:, 0:32], L1, T.Msk[:, :], False, False)
+    PE.matmul(T.b3[:, 0:16], L1, T.Msk[:, 16:32], False, False)
+    PE.matmul(T.b3[:, 16:32], L1B, T.Msk[:, 0:16], False, False)
+    wait("p", v_sc)
+    PE.matmul(T.b3[:, 0:16], ONE, T.Sc[:, :], False, False)
+    PE.matmul(T.b3[:, 16:32], ONE, T.Sc[:, :], False, False)
+    wait("p", v_mj)
+    p_pos = ev(PE.matmul(T.b3[:, 0:32], NIP, T.MJ[:, :], False, True))
+    p_nt = ev(PE.matmul(T.b7[:, 256:257], ONE, T.Sc[:, 15:16], True, True))
+    wait("v", v_kx)
+    v_kf2 = ev(V.tensor_copy(T.kxf[:, :], T.kx[:, :]))
+    m_yy = ev(V.memset(T.YY[:, :], 0.0))
+    wait("v", v_kf2, m_yy)
+    v_yy = ev(V.tensor_scalar(out=T.YY[:, 15:143:16], in0=T.row2d[:, :], scalar1=T.kxf[:, :], scalar2=None,
+                              op0=A.is_equal))
+    wait("v", p_pos)
+    v_o3 = ev(V.tensor_copy(T.off3[:, :], T.b3[:, 0:32]))
+    wait("s", p_nt)
+    s_nt = ev(S.activation(T.nt[:, :], T.b7[:, 256:257], AF.Copy))
+
+    wait("v", v_o3, s_k1, z_w1)
+    v_w1 = ev(V.tensor_copy(T.W1[:, :].indirect(T.off3[:, :]), T.K1[:, :]))
+    wait("v", s_mer, z_wm)
+    v_wm = ev(V.tensor_copy(T.Wm[:, :].indirect(T.off3[:, 0:16]), T.MeR[:, 0:256]))
+    wait("p", v_w1, v_yy)
+    for i in range(16):
+        last = PE.matmul(T.b4[:, 0:96], T.YY[:, 15 - i:143 - i], T.W1[:, i:C:16], i == 0, i == 15)
+    p_l = ev(last)
+    wait("v", p_l)
+    v_lu = ev(V.tensor_scalar(out=T.Lu[:, :], in0=T.b4[:, 0:96], scalar1=8192.0, scalar2=None, op0=A.add))
+    wait("g", v_lu)
+    send("h2_%d" % q, lambda r: T.Lu[:, :], T.Lr[:, 96 * q:96 * q + 96])
+    wait("g", s_nt)
+    ev(g.dma_start(T.y[:, C:C + 1], T.nt[0:16, :], allow_slow_non_contiguous=True), 16)
+    wait("v", v_wm)
+    v_wm2 = ev(V.tensor_copy(T.Wm[:, :].indirect(T.off3[:, 16:32]), T.MeR[:, 256:512]))
+
+    wait("v", v_lu)
+    v_o2 = ev(V.tensor_copy(T.off2[32 * q:32 * q + 32, :], T.Lu[32 * q:32 * q + 32, :]))
+    for r in order:
+        wait("v", "h2_%d" % r)
+        ev(V.tensor_copy(T.off2[32 * r:32 * r + 32, :], T.Lr[32 * q:32 * q + 32, 96 * r:96 * r + 96]), 1, v_o2)
+    wait("v", v_o2, d_at, m_w)
+    wait("p", c_sel)
+    pa, pb = new(), [new(), new()]
+    for c in range(8):
+        e = ev(V.tensor_copy(T.G[:, 128 * c:128 * c + 128], T.ATW[:, :].indirect(T.off2[:, 8 * c:8 * c + 8])))
+        wait("p", e)
+        ev(PE.matmul(T.b5[:, c:512:8], T.G[:, 128 * c:128 * c + 128], T.sele[:, :], True, True), 1, pa)
+    for c in (8, 10):
+        e = ev(V.tensor_copy(T.G[:, 128 * c:128 * c + 256], T.ATW[:, :].indirect(T.off2[:, 8 * c:8 * c + 16])))
+        wait("p", e)
+        for ch in range(2):
+            k = c // 2 - 4
+            ev(PE.matmul((T.b6 if ch == 0 else T.b2)[:, k:128:2], T.G[:, 128 * c + ch:128 * c + 256:2], T.sele[:, :],
+                         True, True), 1, pb[ch])
+    wait("s", pa)
+    s_sa = ev(S.activation(T.SA[:, :], T.b5[:, :], AF.Copy))
+    wait("g", s_sa)
+    send("h3a_%d" % q, lambda r: T.SA[:, 128 * r:128 * r + 128], T.LA[:, 128 * q:128 * q + 128])
+    wait("p", v_wm2, s_nt)
+    p_m = new()
+    for c in range(12):
+        o = T.b7[:, c:128:8]
+        l = T.Wm[:, 128 * c:128 * c + 128]
+        if c >= 8:
+            k, ch = (c - 8) // 2, c % 2
+            o = T.b7[:, 128 + 32 * ch + k:160 + 32 * ch:2]
+            l = T.Wm[:, 1024 + 256 * k + ch:1280 + 256 * k:2]
+        ev(PE.matmul(o, l, T.onesb[:, 0:16], True, True), 1, p_m)
+    SB, LB, ps_b = [T.SB0, T.SB1], [T.LB0, T.LB1], [T.b6, T.b2]
+    v_sb = []
+    for ch in range(2):
+        wait("v", pb[ch])
+        v_sb.append(ev(V.transpose(SB[ch][:, :], ps_b[ch][:, 0:128])))
+        wait("g", v_sb[ch])
+        b = SB[ch]
+        send("h3b%d_%d" % (ch, q), lambda r: b[:, 32 * r:32 * r + 32], LB[ch][:, 32 * q:32 * q + 32])
+
+    mA = T.b7[:, 0:128]
+    wait("v", p_m)
+    t = ev(V.transpose(T.tB[:, :], T.b7[:, 128:192]))
+    wait("v", s_sa)
+    a = ev(V.tensor_tensor(mA, mA, T.SA[:, 128 * q:128 * q + 128], A.add))
+    x = []
+    wait("v", t, *v_sb)
+    for ch in range(2):
+        o = T.tB[:, 32 * ch:32 * ch + 32]
+        x.append(ev(V.tensor_tensor(o, o, SB[ch][:, 32 * q:32 * q + 32], A.add)))
+    for r in order:
+        wait("v", "h3a_%d" % r, a)
+        o = T.accA[:, :] if r == order[-1] else mA
+        a = ev(V.tensor_tensor(o, mA, T.LA[:, 128 * r:128 * r + 128], A.add))
+    wait("p", a, c_idf)
+    p_a = ev(PE.matmul(T.b0[:, 0:128], T.accA[:, :], T.idf[:, :], True, True))
+    wait("s", p_a)
+    s_oa = ev(S.activation(T.OA[:, :], T.b0[:, 0:128], AF.Copy))
+    wait("y", s_oa)
+    ev(SY.dma_start(T.y[:, 0:1024], T.OA[:, :]), 16)
+    for r in order:
+        for ch in range(2):
+            wait("v", "h3b%d_%d" % (ch, r), x[ch])
+            i = T.tB[:, 32 * ch:32 * ch + 32]
+            o = T.OB[:, ch:64:2] if r == order[-1] else i
+            x[ch] = ev(V.tensor_tensor(o, i, LB[ch][:, 32 * r:32 * r + 32], A.add))
+    for n, k in (("y", 0), ("s", 1)):
+        wait(n, *x)
+        for b in range(4):
+            ev(queues[n].dma_start(T.y[:, 1024 + 256 * k + 64 * b:1088 + 256 * k + 64 * b],
+                                   T.OB[32 * b + k:32 * b + 32:2, :]), 16)
+
+    for s in total:
+        if waited.get(s, 0) < total[s]:
+            wait("g", s)

@@ -3,9 +3,10 @@ from concourse.mybir import AluOpType as A, ActivationFunctionType as AF
 import numpy as np
 
 R, F, C, D, NR = 8192, 4096, 1536, 2, 4
-TR = 3584
 EARLY = 2
 P1, P2 = 2560, 4608
+PAD = 8
+ROUND = 1.5 * 2.0 ** 32
 
 SCRATCH = {
     "limi": ("sbuf", [128, 2], "int32"), "limf": ("sbuf", [128, 2], "float32"),
@@ -15,38 +16,38 @@ SCRATCH = {
     "fkt": ("sbuf", [128, 256], "int32"), "off16": ("sbuf", [128, 256], "uint16"),
     "fhi": ("sbuf", [128, 256], "int32"), "flo": ("sbuf", [128, 256], "int32"),
     "fhib": ("sbuf", [128, 256], "bfloat16"), "flob": ("sbuf", [128, 256], "bfloat16"),
-    "K1": ("sbuf", [128, 512], "bfloat16"), "W1": ("sbuf", [128, TR], "bfloat16"),
+    "K1": ("sbuf", [128, 512], "bfloat16"), "W1": ("sbuf", [128, 3584], "bfloat16"),
+    "W2": ("sbuf", [128, 3, 4, 4, 2, 16], "bfloat16"),
     "mei": ("sbuf", [128, 32], "int32"), "mep": ("sbuf", [128, 96], "int32"),
-    "MEL": ("sbuf", [128, 512], "bfloat16"), "MeR": ("sbuf", [128, 512], "bfloat16"),
-    "Wm": ("sbuf", [128, TR], "bfloat16"),
+    "MEL": ("sbuf", [128, 512], "bfloat16"),
     "onesb": ("sbuf", [128, 128], "bfloat16"), "onesf": ("sbuf", [128, 128], "float32"),
     "zb": ("sbuf", [128, 128], "bfloat16"),
-    "limsel": ("sbuf", [128, 128], "float32"), "Qt": ("sbuf", [128, 260], "bfloat16"),
-    "YY": ("sbuf", [128, 144], "bfloat16"), "kc": ("sbuf", [128, 1], "int32"),
-    "kx": ("sbuf", [128, 1], "int32"), "kxf": ("sbuf", [128, 1], "float32"),
+    "limsel": ("sbuf", [128, 128], "float32"),
+    "Qlo": ("sbuf", [128, 256], "bfloat16"), "Qhi": ("sbuf", [128, 256], "bfloat16"),
+    "kc": ("sbuf", [128, 1], "int32"), "ke": ("sbuf", [128, 1], "int32"), "kef": ("sbuf", [128, 1], "float32"),
     "ku": ("sbuf", [128, 1], "int32"), "kuf": ("sbuf", [128, 1], "float32"),
-    "row2d": ("sbuf", [128, 8], "float32"), "rowj": ("sbuf", [128, 32], "float32"),
-    "J": ("sbuf", [128, 32], "float16"),
+    "rowj": ("sbuf", [128, 32], "float32"), "J": ("sbuf", [128, 32], "float16"),
     "mats": ("sbuf", [128, 384], "bfloat16"), "H": ("sbuf", [128, 640], "float16"),
-    "idb": ("sbuf", [128, 128], "bfloat16"), "idf": ("sbuf", [128, 128], "float32"),
-    "sele": ("sbuf", [128, 64], "float32"),
+    "idb": ("sbuf", [128, 128], "bfloat16"), "sele": ("sbuf", [128, 64], "float32"),
+    "rep": ("sbuf", [128, 128], "bfloat16"), "R16": ("sbuf", [128, 16], "bfloat16"),
+    "RL": ("sbuf", [128, 16], "bfloat16"), "RM": ("sbuf", [128, 16], "bfloat16"),
+    "rm3": ("sbuf", [128, 4], "float32"), "rm1": ("sbuf", [128, 1], "float32"),
     "Msk": ("sbuf", [128, 32], "float16"), "Sc": ("sbuf", [128, 16], "float16"),
     "MJ": ("sbuf", [128, 32], "float16"), "off3": ("sbuf", [128, 32], "uint16"),
     "nt": ("sbuf", [128, 1], "float32"),
-    "Lu": ("sbuf", [128, 96], "uint16"), "Lr": ("sbuf", [128, NR * 96], "uint16"),
-    "off2": ("sbuf", [128, 96], "uint16"),
-    "ATW": ("sbuf", [128, R + 8], "int32"), "G": ("sbuf", [128, C], "float32"),
-    "SA": ("sbuf", [128, 512], "float32"), "LA": ("sbuf", [128, 512], "float32"),
-    "SB0": ("sbuf", [128, 128], "float32"), "LB0": ("sbuf", [128, 128], "float32"),
-    "SB1": ("sbuf", [128, 128], "float32"), "LB1": ("sbuf", [128, 128], "float32"),
-    "accA": ("sbuf", [128, 128], "float32"), "tB": ("sbuf", [128, 64], "float32"),
-    "OA": ("sbuf", [128, 128], "float32"), "OB": ("sbuf", [128, 64], "float32"),
+    "Z": ("sbuf", [128, 48], "float32"), "T2": ("sbuf", [128, 96], "float32"),
+    "Ls": ("sbuf", [128, 24, 2, 2], "uint16"), "Lr": ("sbuf", [128, NR * 24], "uint16"),
+    "ATW": ("sbuf", [128, R + PAD], "int32"), "G": ("sbuf", [128, C], "float32"),
+    "S0": ("sbuf", [128, 192], "float32"), "S1": ("sbuf", [128, 192], "float32"), "S2": ("sbuf", [128, 192], "float32"),
+    "L0": ("sbuf", [128, 192], "float32"), "L1": ("sbuf", [128, 192], "float32"),
+    "L2": ("sbuf", [128, 6, 2, 16], "float32"), "O": ("sbuf", [128, 192], "float32"),
+    "bT": ("psum", [128, 16, 2, 16], "float32"),
 }
-for _b in range(8):
+for _b in (0, 1, 2, 3, 4, 5, 7):
     SCRATCH["b%d" % _b] = ("psum", [128, 512], "float32")
-NEV = 122
-SEMAPHORES = (["e%d" % _i for _i in range(NEV)] + ["left", "h1"]
-              + ["%s_%d" % (_n, _q) for _n in ("h2", "h3a", "h3b0", "h3b1") for _q in range(NR)])
+NEV = 135
+SEMAPHORES = (["e%d" % _i for _i in range(NEV)] + ["left", "h1", "h3_0", "h3_1", "h3_2"]
+              + ["h2_%d" % _q for _q in range(NR)])
 
 
 def rank_program(g, core, T, topo):
@@ -77,30 +78,30 @@ def rank_program(g, core, T, topo):
                 seen[(k, s)] = n
                 waited[s] = max(waited.get(s, 0), n)
 
-    others = [c for c in T.cores if c != core]
-    cross = [c for c in others if topo.die(c) != topo.die(core)]
-    same = [c for c in others if topo.die(c) == topo.die(core)]
-    dests = cross[:1] + same + cross[1:]
-    order = [T.rank_of(c) for c in dests]
+    mine = [c for c in T.cores if topo.die(c) == topo.die(core)]
+    far = [c for c in T.cores if topo.die(c) != topo.die(core)]
+    at = mine.index(core)
+    partners = [far[at], far[1 - at], mine[1 - at]]
+    order = [T.rank_of(c) for c in partners]
     total["h1"] = 12
-    for n in ("h2", "h3a", "h3b0", "h3b1"):
-        for r in order:
-            total["%s_%d" % (n, r)] = 4
+    for r in order:
+        total["h2_%d" % r] = 4
+    for k in range(3):
+        total["h3_%d" % k] = 16
 
-    def send(rsem, src, dst):
-        tr = []
-        for k, c in enumerate(dests):
-            rid, pid, _ = topo.addr(c)
-            mask = sum(1 << e for e in topo.engines(core, c)[k::4])
-            tr.append(RemoteDMATransfer(dst_ids=[DstId(rid=rid, pnc=pid)], dma_engine_mask=mask,
-                                        remote_sem=T.sem[rsem], src=src(T.rank_of(c)), dst=dst))
-        g.remote_dma_fused(tr, local_sem=T.sem.left)
-        total["left"] = total.get("left", 0) + 4 * len(dests)
+    def transfer(c, engines, rsem, src, dst):
+        rid, pid, _ = topo.addr(c)
+        total["left"] = total.get("left", 0) + len(engines)
+        return RemoteDMATransfer(dst_ids=[DstId(rid=rid, pnc=pid)], dma_engine_mask=sum(1 << e for e in engines),
+                                 remote_sem=T.sem[rsem], src=src, dst=dst)
+
+    def send_all(rsem, src, dst):
+        g.remote_dma_fused([transfer(c, topo.engines(core, c)[k::4], rsem, src(T.rank_of(c)), dst)
+                            for k, c in enumerate([partners[0], partners[2], partners[1]])], local_sem=T.sem.left)
 
     def at_load(k):
-        r, e = k // 2, k % 2
-        p = 32 * r + 16 * e
-        return SY.dma_start(T.ATW[p:p + 16, 0:R], T.at[:, R * e:R * e + R])
+        e = k // 4
+        return SY.dma_start(T.ATW[16 * k:16 * k + 16, PAD:PAD + R], T.at[:, R * e:R * e + R])
 
     d_lim = ev(SY.dma_start(T.limi[0:2, :], T.lim[0:1, :]), 16)
     d_a0 = ev(S.dma_start(T.a0[:, :], T.at[0:1, :]), 16)
@@ -115,7 +116,7 @@ def rank_program(g, core, T, topo):
     m_one = ev(V.memset(T.onesf[:, :], 1.0))
     ev(V.memset(T.onesb[:, :], 1.0), 1, m_one)
     m_z = ev(V.memset(T.zb[:, :], 0.0))
-    ev(V.memset(T.Qt[:, :], 0.0), 1, m_z)
+    ev(V.memset(T.Qhi[:, :], 0.0), 1, m_z)
     z1 = ev(V.memset(T.pw[:, 1024:P1], 0.0))
     wait("s", z0)
     z2 = new()
@@ -123,16 +124,14 @@ def rank_program(g, core, T, topo):
         n = min(1024, R - k)
         ev(S.activation(T.pw[:, k:k + n], T.pw[:, 0:n], AF.Copy), 1, z2)
 
+    c_io = ev(g.iota(T.kc[:, :], [[0, 1]], 0, 1))
+    ev(g.iota(T.rowj[:, :], [[1, 2], [32, 16]], C, 0, allow_small_or_imprecise_dtypes=True), 1, c_io)
     wait("g", m_one)
     c_lim = ev(g.affine_select(T.limsel[0:2, :], T.onesf[0:2, :], [[1, 2], [0, 64]], A.is_equal, 0.0, 0, -1))
-    wait("g", m_z)
     c_q = new()
     for h in range(2):
-        ev(g.affine_select(T.Qt[:, 130 * h + 1:130 * h + 129:2], T.onesb[:, 0:64], [[2, 8], [16, 8]],
+        ev(g.affine_select(T.Qlo[:, 128 * h:128 * h + 128], T.onesb[:, :], [[2, 8], [16, 16]],
                            A.is_equal, 0.0, h, -1), 1, c_q)
-    c_io = ev(g.iota(T.kc[:, :], [[0, 1]], 0, 1))
-    ev(g.iota(T.row2d[:, :], [[2, 8]], 0, 0, allow_small_or_imprecise_dtypes=True), 1, c_io)
-    ev(g.iota(T.rowj[:, :], [[1, 2], [32, 16]], C, 0, allow_small_or_imprecise_dtypes=True), 1, c_io)
 
     wait("v", d_lim)
     v_lim = ev(V.tensor_copy(T.limf[0:2, :], T.limi[0:2, :]))
@@ -144,7 +143,7 @@ def rank_program(g, core, T, topo):
     wait("v", v_cl)
     v_ps = ev(V.tensor_tensor(T.ps[:, :], T.b2[:, 128:256], T.a0[:, :], A.is_equal))
     wait("g", v_ps)
-    send("h1", lambda r: T.ps[:, :], T.PD[q])
+    send_all("h1", lambda r: T.ps[:, :], T.PD[q])
     ev(V.memset(T.pw[:, P1:P2], 0.0), 1, z1)
     wait("y", v_ps, z0, z1, z2)
     d_pw = ev(SY.dma_start(T.pw[32 * q:32 * q + 32:16, :], T.ps[:, :]), 16)
@@ -155,64 +154,81 @@ def rank_program(g, core, T, topo):
     for k in range(EARLY, 8):
         ev(at_load(k), 16, d_at)
 
-    wait("v", d_fk)
-    v_off = ev(V.tensor_copy(T.off16[:, :], T.fkt[:, :]))
-    v_k = ev(V.tensor_scalar(out=T.fhi[:, :], in0=T.fkt[:, :], scalar1=0x1F80, scalar2=None, op0=A.bitwise_and))
-    ev(V.tensor_scalar(out=T.flo[:, :], in0=T.fkt[:, :], scalar1=127, scalar2=None, op0=A.bitwise_and), 1, v_k)
-    wait("v", v_k)
-    v_kb = ev(V.tensor_scalar(out=T.fhib[:, :], in0=T.fhi[:, :], scalar1=-8192.0, scalar2=None, op0=A.add))
-    ev(V.tensor_copy(T.flob[:, :], T.flo[:, :]), 1, v_kb)
-    wait("p", v_kb, c_q)
-    p_r = new()
+    wait("g", m_z)
+    c_h0, c_h = new(), new()
     for h in range(2):
-        o = T.b0[:, 256 * h:256 * h + 256]
-        ev(PE.matmul(o, T.Qt[:, 130 * h + 1:130 * h + 129], T.fhib[:, :], True, False), 1, p_r)
-        ev(PE.matmul(o, T.Qt[:, 130 * h:130 * h + 128], T.flob[:, :], False, True), 1, p_r)
-    wait("s", p_r)
-    s_k1 = ev(S.activation(T.K1[:, :], T.b0[:, :], AF.Copy))
-
+        ev(g.affine_select(T.Qhi[:, 128 * h:128 * h + 128:2], T.onesb[:, 0:64], [[2, 8], [32, 8]],
+                           A.is_equal, 0.0, h - 128, -1), 1, c_h0)
     c_idb = ev(g.affine_select(T.idb[:, :], T.onesb[:, :], [[1, 128]], A.is_equal, 0.0, 0, -1))
+    wait("g", c_h0)
+    ev(g.affine_select(T.Qhi[:, 0:256:2], T.Qhi[:, 0:256:2], [[1, 2], [2, 8], [32, 8]],
+                       A.not_equal, 1.0, 16 - 128, -1), 1, c_h)
     c_m = new()
     pat = [[1, 8], [8, 16]]
     ev(g.affine_select(T.mats[:, 0:128], T.zb[:, :], pat, A.is_gt, -1.0, 0, -1), 1, c_m)
     ev(g.affine_select(T.mats[:, 128:256], T.zb[:, :], pat, A.is_ge, -1.0, 0, -1), 1, c_m)
     ev(g.affine_select(T.mats[:, 256:384], T.onesb[:, :], pat, A.is_equal, 0.0, 0, -1), 1, c_m)
     z_w1 = ev(g.iota(T.W1[:, 0:C], [[0, C]], 0, 0, allow_small_or_imprecise_dtypes=True))
-    c_s1 = ev(g.affine_select(T.sele[:, :], T.onesf[:, 0:64], [[32, 4], [1, 16]], A.is_equal, 0.0, 0, -1))
-    c_idf = ev(g.affine_select(T.idf[:, :], T.onesf[:, :], [[1, 128]], A.is_equal, 0.0, 0, -1))
+    c_r = ev(g.affine_select(T.R16[0:16, :], T.onesb[0:16, 0:16], [[8, 2], [1, 2], [2, 4]], A.is_equal, 0.0, 0, -1))
+    c_rep = ev(g.affine_select(T.rep[0:16, :], T.onesb[0:16, :], [[0, 8], [1, 16]], A.is_equal, 0.0, 0, -1))
+    wait("g", c_r)
+    c_r = ev(g.affine_select(T.R16[0:16, 0:4], T.R16[0:16, 0:4], [[2, 4]], A.not_equal, 1.0, 8, -1))
+    for lo, w in ((4, 256.0 + PAD), (8, -240.0)):
+        ev(g.affine_select(T.R16[0:16, lo:lo + 4], T.R16[0:16, lo:lo + 4], [[0, 4]], A.not_equal, w, 15, -1), 1, c_rep)
+    c_s1 = ev(g.affine_select(T.sele[:, :], T.onesf[:, 0:64], [[16, 2], [1, 16], [32, 2]], A.is_equal, 0.0, 0, -1))
+    wait("g", c_r)
+    ev(g.affine_select(T.R16[0:16, 0:4], T.R16[0:16, 0:4], [[0, 4]], A.not_equal, (256.0 + PAD) / 16, 15, -1), 1, c_rep)
     wait("g", c_s1)
-    c_sel = ev(g.affine_select(T.sele[:, :], T.sele[:, :], [[32, 4], [1, 16]], A.not_equal, 1.0, 16, -1))
+    c_sel = ev(g.affine_select(T.sele[:, :], T.sele[:, :], [[16, 2], [1, 16], [32, 2]], A.not_equal, 1.0, 64, -1))
 
-    m_w = ev(V.memset(T.ATW[:, R:R + 8], 0))
+    wait("v", d_fk, c_io)
+    v_off = ev(V.tensor_copy(T.off16[:, :], T.fkt[:, :]))
+    v_k = ev(V.tensor_scalar(out=T.ke[:, :], in0=T.kc[:, :], scalar1=16, scalar2=None, op0=A.bitwise_and))
+    v_ku = ev(V.tensor_scalar(out=T.ku[:, :], in0=T.kc[:, :], scalar1=3, scalar2=None, op0=A.arith_shift_right))
+    v_k2 = ev(V.tensor_scalar(out=T.fhi[:, :], in0=T.fkt[:, :], scalar1=0x1E00, scalar2=None, op0=A.bitwise_and))
+    wait("v", v_k)
+    ev(V.tensor_scalar(out=T.kef[:, :], in0=T.ke[:, :], scalar1=15.0 / 256, scalar2=1.0 / 16, op0=A.mult, op1=A.add),
+       1, v_k2)
+    ev(V.tensor_scalar(out=T.flo[:, :], in0=T.fkt[:, :], scalar1=511, scalar2=None, op0=A.bitwise_and), 1, v_k2)
+    wait("v", v_k2)
+    v_kb = ev(V.tensor_scalar(out=T.fhib[:, :], in0=T.fhi[:, :], scalar1=T.kef[:, :], scalar2=None, op0=A.mult))
+    ev(V.tensor_scalar(out=T.flob[:, :], in0=T.flo[:, :], scalar1=-256.0, scalar2=T.kef[:, :], op0=A.add, op1=A.mult),
+       1, v_kb)
+
+    m_w = ev(V.memset(T.ATW[:, 0:PAD], 0))
     m_mel = ev(V.memset(T.MEL[:, :], 0.0))
-    wait("v", d_me, c_io)
+    wait("v", d_me)
     v_mp = ev(V.tensor_scalar(out=T.mep[:, 0:32], in0=T.mei[:, :], scalar1=14, scalar2=None, op0=A.arith_shift_right))
     ev(V.tensor_scalar(out=T.mep[:, 32:64], in0=T.mei[:, :], scalar1=0x3F80, scalar2=None, op0=A.bitwise_and), 1, v_mp)
     ev(V.tensor_scalar(out=T.mep[:, 64:96], in0=T.mei[:, :], scalar1=127, scalar2=None, op0=A.bitwise_and), 1, v_mp)
-    v_ku = ev(V.tensor_scalar(out=T.ku[:, :], in0=T.kc[:, :], scalar1=3, scalar2=None, op0=A.arith_shift_right))
-    v_kx = ev(V.tensor_scalar(out=T.kx[:, :], in0=T.kc[:, :], scalar1=14, scalar2=None, op0=A.bitwise_and))
-    wait("v", v_mp, m_mel)
-    v_mel = new()
+    wait("v", m_mel)
+    v_mel = ev(V.memset(T.MEL[:, 15:512:16], 1.0))
+    wait("v", v_mp)
     for x in range(3):
         for h in range(2):
-            ev(V.tensor_scalar(out=T.MEL[:, 256 * h + x:256 * h + 256:16], in0=T.mep[:, 32 * x + h:32 * x + 32:2],
+            ev(V.tensor_scalar(out=T.MEL[:, 256 * h + 9 + 2 * x:256 * h + 256:16],
+                               in0=T.mep[:, 32 * x + h:32 * x + 32:2],
                                scalar1=16384.0 if x == 0 else 1.0, scalar2=None, op0=A.mult), 1, v_mel)
     wait("v", v_ku)
     v_kf = ev(V.tensor_scalar(out=T.kuf[:, :], in0=T.ku[:, :], scalar1=2.0, scalar2=None, op0=A.mult))
-    wait("p", v_mel, c_idb)
-    p_me = new()
-    for x in range(4):
-        ev(PE.matmul(T.b1[:, 128 * x:128 * x + 128], T.MEL[:, 128 * x:128 * x + 128], T.idb[:, :], True, True), 1, p_me)
+    wait("p", v_kb, c_q, c_h, v_mel, c_idb)
+    p_r = new()
+    for h in range(2):
+        o = T.b0[:, 256 * h:256 * h + 256]
+        PE.matmul(o, T.Qlo[:, 128 * h:128 * h + 128], T.flob[:, :], True, False)
+        PE.matmul(o, T.Qhi[:, 128 * h:128 * h + 128], T.fhib[:, :], False, False)
+        for x in range(2 * h, 2 * h + 2):
+            last = PE.matmul(T.b0[:, 128 * x:128 * x + 128], T.MEL[:, 128 * x:128 * x + 128], T.idb[:, :],
+                             False, x % 2 == 1)
+        ev(last, 1, p_r)
 
     wait("v", d_pw, v_off, z0, z1)
     wait("s", d_pw, v_off, z0, z1)
     p_c = new()
-    vgot = []
     for lo, hi in ((0, 3), (3, 5), (5, 7), (7, 8)):
         got = [ev(V.tensor_copy(T.Pg[:, 256 * lo:256 * hi], T.pw[:, :].indirect(T.off16[:, 16 * lo:16 * hi]))),
                ev(S.activation(T.Pg[:, 2048 + 256 * lo:2048 + 256 * hi],
                                T.pw[:, :].indirect(T.off16[:, 128 + 16 * lo:128 + 16 * hi]), AF.Copy))]
-        vgot.append(got[0])
         for b in range(2):
             wait("p", got[b])
             for uh in range(8 * b + lo, 8 * b + hi):
@@ -220,10 +236,8 @@ def rank_program(g, core, T, topo):
                     w = 16 * h + uh
                     ev(PE.matmul(T.b2[:, w:w + 1], T.Pg[:, 256 * uh + h:256 * uh + 256:2], T.onesb[:, 0:1], True, True),
                        1, p_c)
-    wait("s", p_me)
-    s_mer = ev(S.activation(T.MeR[:, :], T.b1[:, :], AF.Copy))
-    wait("s", *vgot)
-    z_wm = ev(S.activation(T.Wm[:, 0:C], T.Pg[:, 0:C], AF.Copy, scale=0.0))
+    wait("s", p_r)
+    s_k1 = ev(S.activation(T.K1[:, :], T.b0[:, :], AF.Copy))
 
     wait("v", c_m, v_kf)
     v_h = ev(V.tensor_copy(T.H[:, 0:384], T.mats[:, :]))
@@ -248,107 +262,112 @@ def rank_program(g, core, T, topo):
     wait("p", v_mj)
     p_pos = ev(PE.matmul(T.b3[:, 0:32], NIP, T.MJ[:, :], False, True))
     p_nt = ev(PE.matmul(T.b7[:, 256:257], ONE, T.Sc[:, 15:16], True, True))
-    wait("v", v_kx)
-    v_kf2 = ev(V.tensor_copy(T.kxf[:, :], T.kx[:, :]))
-    m_yy = ev(V.memset(T.YY[:, :], 0.0))
-    wait("v", v_kf2, m_yy)
-    v_yy = ev(V.tensor_scalar(out=T.YY[:, 15:143:16], in0=T.row2d[:, :], scalar1=T.kxf[:, :], scalar2=None,
-                              op0=A.is_equal))
+    wait("p", c_rep)
+    p_rl = ev(PE.matmul(T.b1[:, 0:16], T.rep[0:16, :], T.R16[0:16, :], True, True))
     wait("v", p_pos)
     v_o3 = ev(V.tensor_copy(T.off3[:, :], T.b3[:, 0:32]))
+    wait("s", p_rl)
+    s_rl = ev(S.activation(T.RL[:, :], T.b1[:, 0:16], AF.Copy))
+    s_r1 = ev(S.activation(T.rm3[:, 0:3], T.b1[:, 12:15], AF.Copy, accum_out=T.rm1[:, :]))
     wait("s", p_nt)
     s_nt = ev(S.activation(T.nt[:, :], T.b7[:, 256:257], AF.Copy))
+    wait("s", s_r1)
+    s_rm = ev(S.activation(T.RM[:, :], T.onesb[:, 0:16], AF.Copy, scale=T.rm1[:, :]))
 
     wait("v", v_o3, s_k1, z_w1)
     v_w1 = ev(V.tensor_copy(T.W1[:, :].indirect(T.off3[:, :]), T.K1[:, :]))
-    wait("v", s_mer, z_wm)
-    v_wm = ev(V.tensor_copy(T.Wm[:, :].indirect(T.off3[:, 0:16]), T.MeR[:, 0:256]))
-    wait("p", v_w1, v_yy)
-    for i in range(16):
-        last = PE.matmul(T.b4[:, 0:96], T.YY[:, 15 - i:143 - i], T.W1[:, i:C:16], i == 0, i == 15)
-    p_l = ev(last)
+    wait("p", v_w1, s_rl)
+    p_l = new()
+    for c in range(6):
+        for j1 in range(2):
+            y = 4 * (c // 2) + 2 * j1 + c % 2
+            ev(PE.matmul(T.b4[:, y:144:12], T.W1[:, 768 * j1 + c:768 * j1 + 768:6], T.RL[:, 0:12], True, True), 1, p_l)
+    wait("s", v_w1)
+    s_w2 = new()
+    for c in range(6):
+        for jb in range(4):
+            ev(S.activation(T.W2[:, c // 2, :, jb, c % 2, :], T.W1[:, 384 * jb + c:384 * jb + 384:6], AF.Copy), 1, s_w2)
     wait("v", p_l)
-    v_lu = ev(V.tensor_scalar(out=T.Lu[:, :], in0=T.b4[:, 0:96], scalar1=8192.0, scalar2=None, op0=A.add))
+    v_z = ev(V.tensor_scalar(out=T.Z[:, :], in0=T.b4[:, 96:144], scalar1=ROUND, scalar2=ROUND, op0=A.add,
+                             op1=A.subtract))
+    wait("v", v_z)
+    v_t = [ev(V.tensor_tensor(T.T2[:, 48 * e:48 * e + 48], T.b4[:, 48 * e:48 * e + 48], T.Z[:, :],
+                              A.add if e else A.subtract)) for e in range(2)]
+    v_lu = new()
+    for e in range(2):
+        wait("v", v_t[e])
+        for j0 in range(2):
+            ev(V.tensor_scalar(out=T.Ls[64 * e:64 * e + 64, :, j0, :], in0=T.T2[64 * j0:64 * j0 + 64, 48 * e:48 * e + 48],
+                               scalar1=1.0 if e else 16.0, scalar2=None, op0=A.mult), 1, v_lu)
     wait("g", v_lu)
-    send("h2_%d" % q, lambda r: T.Lu[:, :], T.Lr[:, 96 * q:96 * q + 96])
+    send_all("h2_%d" % q, lambda r: T.Ls[:, 6 * r:6 * r + 6, :, :], T.Lr[:, 24 * q:24 * q + 24])
     wait("g", s_nt)
     ev(g.dma_start(T.y[:, C:C + 1], T.nt[0:16, :], allow_slow_non_contiguous=True), 16)
-    wait("v", v_wm)
-    v_wm2 = ev(V.tensor_copy(T.Wm[:, :].indirect(T.off3[:, 16:32]), T.MeR[:, 256:512]))
 
     wait("v", v_lu)
-    v_o2 = ev(V.tensor_copy(T.off2[32 * q:32 * q + 32, :], T.Lu[32 * q:32 * q + 32, :]))
-    for r in order:
-        wait("v", "h2_%d" % r)
-        ev(V.tensor_copy(T.off2[32 * r:32 * r + 32, :], T.Lr[32 * q:32 * q + 32, 96 * r:96 * r + 96]), 1, v_o2)
-    wait("v", v_o2, d_at, m_w)
-    wait("p", c_sel)
-    pa, pb = new(), [new(), new()]
-    for c in range(8):
-        e = ev(V.tensor_copy(T.G[:, 128 * c:128 * c + 128], T.ATW[:, :].indirect(T.off2[:, 8 * c:8 * c + 8])))
-        wait("p", e)
-        ev(PE.matmul(T.b5[:, c:512:8], T.G[:, 128 * c:128 * c + 128], T.sele[:, :], True, True), 1, pa)
-    for c in (8, 10):
-        e = ev(V.tensor_copy(T.G[:, 128 * c:128 * c + 256], T.ATW[:, :].indirect(T.off2[:, 8 * c:8 * c + 16])))
-        wait("p", e)
-        for ch in range(2):
-            k = c // 2 - 4
-            ev(PE.matmul((T.b6 if ch == 0 else T.b2)[:, k:128:2], T.G[:, 128 * c + ch:128 * c + 256:2], T.sele[:, :],
-                         True, True), 1, pb[ch])
-    wait("s", pa)
-    s_sa = ev(S.activation(T.SA[:, :], T.b5[:, :], AF.Copy))
-    wait("g", s_sa)
-    send("h3a_%d" % q, lambda r: T.SA[:, 128 * r:128 * r + 128], T.LA[:, 128 * q:128 * q + 128])
-    wait("p", v_wm2, s_nt)
-    p_m = new()
-    for c in range(12):
-        o = T.b7[:, c:128:8]
-        l = T.Wm[:, 128 * c:128 * c + 128]
-        if c >= 8:
-            k, ch = (c - 8) // 2, c % 2
-            o = T.b7[:, 128 + 32 * ch + k:160 + 32 * ch:2]
-            l = T.Wm[:, 1024 + 256 * k + ch:1280 + 256 * k:2]
-        ev(PE.matmul(o, l, T.onesb[:, 0:16], True, True), 1, p_m)
-    SB, LB, ps_b = [T.SB0, T.SB1], [T.LB0, T.LB1], [T.b6, T.b2]
-    v_sb = []
-    for ch in range(2):
-        wait("v", pb[ch])
-        v_sb.append(ev(V.transpose(SB[ch][:, :], ps_b[ch][:, 0:128])))
-        wait("g", v_sb[ch])
-        b = SB[ch]
-        send("h3b%d_%d" % (ch, q), lambda r: b[:, 32 * r:32 * r + 32], LB[ch][:, 32 * q:32 * q + 32])
+    v_own = ev(V.tensor_copy(T.Lr[:, 24 * q:24 * q + 24], T.Ls[:, 6 * q:6 * q + 6, :, :]))
+    wait("v", v_own, d_at, m_w)
+    wait("p", c_sel, s_rm, s_nt, s_k1)
+    SB, LB = [T.S0, T.S1, T.S2], [T.L0, T.L1, T.L2]
 
-    mA = T.b7[:, 0:128]
-    wait("v", p_m)
-    t = ev(V.transpose(T.tB[:, :], T.b7[:, 128:192]))
-    wait("v", s_sa)
-    a = ev(V.tensor_tensor(mA, mA, T.SA[:, 128 * q:128 * q + 128], A.add))
-    x = []
-    wait("v", t, *v_sb)
-    for ch in range(2):
-        o = T.tB[:, 32 * ch:32 * ch + 32]
-        x.append(ev(V.tensor_tensor(o, o, SB[ch][:, 32 * q:32 * q + 32], A.add)))
-    for r in order:
-        wait("v", "h3a_%d" % r, a)
-        o = T.accA[:, :] if r == order[-1] else mA
-        a = ev(V.tensor_tensor(o, mA, T.LA[:, 128 * r:128 * r + 128], A.add))
-    wait("p", a, c_idf)
-    p_a = ev(PE.matmul(T.b0[:, 0:128], T.accA[:, :], T.idf[:, :], True, True))
-    wait("s", p_a)
-    s_oa = ev(S.activation(T.OA[:, :], T.b0[:, 0:128], AF.Copy))
-    wait("y", s_oa)
-    ev(SY.dma_start(T.y[:, 0:1024], T.OA[:, :]), 16)
-    for r in order:
-        for ch in range(2):
-            wait("v", "h3b%d_%d" % (ch, r), x[ch])
-            i = T.tB[:, 32 * ch:32 * ch + 32]
-            o = T.OB[:, ch:64:2] if r == order[-1] else i
-            x[ch] = ev(V.tensor_tensor(o, i, LB[ch][:, 32 * r:32 * r + 32], A.add))
-    for n, k in (("y", 0), ("s", 1)):
-        wait(n, *x)
-        for b in range(4):
-            ev(queues[n].dma_start(T.y[:, 1024 + 256 * k + 64 * b:1088 + 256 * k + 64 * b],
-                                   T.OB[32 * b + k:32 * b + 32:2, :]), 16)
+    def gather(r, lo, hi, out):
+        e = ev(V.tensor_copy(T.G[:, 384 * r + 128 * lo:384 * r + 128 * hi],
+                             T.ATW[:, :].indirect(T.Lr[:, 24 * r + 8 * lo:24 * r + 8 * hi])))
+        wait("p", e)
+        done = new()
+        for ch in range(lo, hi):
+            last = PE.matmul(out[:, 64 * ch:64 * ch + 64], T.G[:, 384 * r + 128 * ch:384 * r + 128 * ch + 128],
+                             T.sele[:, :], True, r != q)
+            if r == q:
+                wait("p", s_w2)
+                for a in range(4):
+                    c0 = 64 * ch + 32 * (a % 2) + a // 2
+                    last = PE.matmul(out[:, c0:c0 + 31:2], T.W2[:, ch, a, :, :, :], T.RM[:, :],
+                                     False, a == 3)
+            ev(last, 1, done)
+        return done
+
+    p_own = gather(q, 0, 3, T.b5)
+    for k in range(2):
+        r = order[k]
+        wait("v", "h2_%d" % r)
+        s = new()
+        for lo, hi, b in (((0, 3, T.b3),), ((0, 2, T.b7), (2, 3, T.b2)))[k]:
+            wait("s", gather(r, lo, hi, b))
+            ev(S.activation(SB[k][:, 64 * lo:64 * hi], b[:, 64 * lo:64 * hi], AF.Copy), 1, s)
+        wait("g", s)
+        g.remote_dma_fused([transfer(partners[k], topo.engines(core, partners[k]), "h3_%d" % k, SB[k][:, :],
+                                     LB[k][:, :])], local_sem=T.sem.left)
+    r = order[2]
+    wait("v", "h2_%d" % r)
+    pa = gather(r, 0, 2, T.b0)
+    wait("p", s_rl, s_r1)
+    pb = gather(r, 2, 3, T.b1)
+    wait("v", pa)
+    v_tr = ev(V.transpose(T.S2[:, 0:128], T.b0[:, 0:128]))
+    wait("v", pb)
+    ev(V.transpose(T.S2[:, 128:192], T.b1[:, 128:192]), 1, v_tr)
+    wait("g", v_tr)
+    g.remote_dma_fused([transfer(partners[2], topo.engines(core, partners[2]), "h3_2", T.S2[:, :], T.L2[:, :, :, :])],
+                       local_sem=T.sem.left)
+
+    acc = T.b5[:, 0:192]
+    a = p_own
+    for k in range(2):
+        wait("v", a, "h3_%d" % k)
+        a = ev(V.tensor_tensor(acc, acc, LB[k][:, :], A.add))
+    wait("v", a)
+    t = ev(V.transpose(T.bT[:, 0:6, :, :], acc))
+    wait("v", t, "h3_2")
+    x = new()
+    for c in range(6):
+        ch, xl = c // 2, c % 2
+        ev(V.tensor_tensor(T.O[:, c:192:6], T.bT[:, 2 * ch:2 * ch + 2, xl, :], T.L2[:, 2 * ch:2 * ch + 2, xl, :], A.add),
+           1, x)
+    for n, jbs in (("y", (0, 1)), ("s", (2, 3))):
+        wait(n, x)
+        for jb in jbs:
+            ev(queues[n].dma_start(T.y[:, 384 * jb:384 * jb + 384], T.O[32 * jb:32 * jb + 32, :]), 16)
 
     for s in total:
         if waited.get(s, 0) < total[s]:

@@ -1,34 +1,36 @@
 from concourse.bass import DstId, RemoteDMATransfer
 from concourse.mybir import AluOpType as A, ActivationFunctionType as AF
-import numpy as np
 
 R, F, C, D, NR = 8192, 4096, 1536, 2, 4
-EARLY = 2
-P1, P2 = 2560, 4608
+PU, PV, PS, PG = 2304, 3072, 5632, 6144
+BULK = (1, 4)
 PAD = 8
+BIG = 1.5 * 2.0 ** 16
 ROUND = 1.5 * 2.0 ** 32
+ROUNDS = ((((0, 32),), ((32, 64),)), (((0, 32),), ((32, 64),)), (((0, 16), (16, 32)), ((48, 64), (32, 48))),
+          (((0, 8), (8, 30)), ((48, 64), (30, 48))))
+BLOCKS = (3, 0, 2, 1)
+WV = 10
 
 SCRATCH = {
-    "limi": ("sbuf", [128, 2], "int32"), "limf": ("sbuf", [128, 2], "float32"),
-    "a0": ("sbuf", [128, 128], "int32"), "ps": ("sbuf", [128, 128], "bfloat16"),
-    "PD": ("dram", [NR, 128, 128], "bfloat16"),
+    "limi": ("sbuf", [128, 4], "int32"), "limb": ("sbuf", [128, 4], "int32"), "limf": ("sbuf", [128, 2], "float32"),
+    "a0": ("sbuf", [128, 256], "int32"), "ps": ("sbuf", [128, 256], "bfloat16"),
     "pw": ("sbuf", [128, R], "bfloat16"), "Pg": ("sbuf", [128, F], "bfloat16"),
-    "fkt": ("sbuf", [128, 256], "int32"), "off16": ("sbuf", [128, 256], "uint16"),
+    "kc": ("sbuf", [128, 1], "int32"), "kb": ("sbuf", [128, 2], "int32"), "kf": ("sbuf", [128, 2], "float32"),
+    "fkt": ("sbuf", [128, 256], "int32"),
+    "KS": ("sbuf", [128, 256], "uint16"), "KR": ("sbuf", [128, 256], "uint16"),
+    "sel4": ("sbuf", [128, 4], "bfloat16"),
+    "CS": ("sbuf", [128, 96], "bfloat16"), "CR": ("sbuf", [128, 96], "bfloat16"), "thr": ("sbuf", [128, 96], "float32"),
     "fhi": ("sbuf", [128, 256], "int32"), "flo": ("sbuf", [128, 256], "int32"),
     "fhib": ("sbuf", [128, 256], "bfloat16"), "flob": ("sbuf", [128, 256], "bfloat16"),
-    "K1": ("sbuf", [128, 512], "bfloat16"), "W1": ("sbuf", [128, 3584], "bfloat16"),
+    "K1": ("sbuf", [128, 512], "bfloat16"), "zb": ("sbuf", [128, 128], "bfloat16"),
     "W2": ("sbuf", [128, 3, 4, 4, 2, 16], "bfloat16"),
-    "mei": ("sbuf", [128, 32], "int32"), "mep": ("sbuf", [128, 96], "int32"),
-    "MEL": ("sbuf", [128, 512], "bfloat16"),
-    "onesb": ("sbuf", [128, 128], "bfloat16"), "onesf": ("sbuf", [128, 128], "float32"),
-    "zb": ("sbuf", [128, 128], "bfloat16"),
-    "limsel": ("sbuf", [128, 128], "float32"),
+    "mei": ("sbuf", [128, 32], "int32"), "mep": ("sbuf", [128, 96], "int32"), "meb": ("sbuf", [128, 96], "bfloat16"),
+    "MEL": ("sbuf", [128, 32, 16], "bfloat16"),
+    "onesb": ("sbuf", [128, 128], "bfloat16"), "idb": ("sbuf", [128, 128], "bfloat16"),
     "Qlo": ("sbuf", [128, 256], "bfloat16"), "Qhi": ("sbuf", [128, 256], "bfloat16"),
-    "kc": ("sbuf", [128, 1], "int32"), "ke": ("sbuf", [128, 1], "int32"), "kef": ("sbuf", [128, 1], "float32"),
-    "ku": ("sbuf", [128, 1], "int32"), "kuf": ("sbuf", [128, 1], "float32"),
-    "rowj": ("sbuf", [128, 32], "float32"), "J": ("sbuf", [128, 32], "float16"),
-    "mats": ("sbuf", [128, 384], "bfloat16"), "H": ("sbuf", [128, 640], "float16"),
-    "idb": ("sbuf", [128, 128], "bfloat16"), "sele": ("sbuf", [128, 64], "float32"),
+    "rowj": ("sbuf", [128, 32], "float32"), "J": ("sbuf", [128, 64], "float16"),
+    "mats": ("sbuf", [128, 384], "bfloat16"), "sele": ("sbuf", [128, 64], "float32"),
     "rep": ("sbuf", [128, 128], "bfloat16"), "R16": ("sbuf", [128, 16], "bfloat16"),
     "RL": ("sbuf", [128, 16], "bfloat16"), "RM": ("sbuf", [128, 16], "bfloat16"),
     "rm3": ("sbuf", [128, 4], "float32"), "rm1": ("sbuf", [128, 1], "float32"),
@@ -45,9 +47,9 @@ SCRATCH = {
 }
 for _b in (0, 1, 2, 3, 4, 5, 7):
     SCRATCH["b%d" % _b] = ("psum", [128, 512], "float32")
-NEV = 135
-SEMAPHORES = (["e%d" % _i for _i in range(NEV)] + ["left", "h1", "h3_0", "h3_1", "h3_2"]
-              + ["h2_%d" % _q for _q in range(NR)])
+NEV = 132
+SEMAPHORES = (["e%d" % _i for _i in range(NEV)] + ["left", "issued", "gone", "sent", "h3_3"]
+              + ["h%d_%d" % (_h, _k) for _h in range(4) for _k in range(3)])
 
 
 def rank_program(g, core, T, topo):
@@ -83,175 +85,244 @@ def rank_program(g, core, T, topo):
     at = mine.index(core)
     partners = [far[at], far[1 - at], mine[1 - at]]
     order = [T.rank_of(c) for c in partners]
-    total["h1"] = 12
-    for r in order:
-        total["h2_%d" % r] = 4
     for k in range(3):
-        total["h3_%d" % k] = 16
+        total["h0_%d" % k] = total["h2_%d" % k] = 8 if k else 16
+        total["h1_%d" % k] = total["h3_%d" % k] = 16
+    total["h3_3"] = 16
 
-    def transfer(c, engines, rsem, src, dst):
+    def transfer(c, engines, rsem, src, dst, left="left"):
         rid, pid, _ = topo.addr(c)
-        total["left"] = total.get("left", 0) + len(engines)
+        total[left] = total.get(left, 0) + len(engines)
         return RemoteDMATransfer(dst_ids=[DstId(rid=rid, pnc=pid)], dma_engine_mask=sum(1 << e for e in engines),
                                  remote_sem=T.sem[rsem], src=src, dst=dst)
 
-    def send_all(rsem, src, dst):
-        g.remote_dma_fused([transfer(c, topo.engines(core, c)[k::4], rsem, src(T.rank_of(c)), dst)
-                            for k, c in enumerate([partners[0], partners[2], partners[1]])], local_sem=T.sem.left)
+    def send(k, rsem, src, dst, left="left"):
+        rid, pid, _ = topo.addr(partners[k])
+        total[left] = total.get(left, 0) + len(topo.engines(core, partners[k]))
+        g.remote_dma(dst, src, T.sem[rsem], T.sem[left], pid, rid, topo.mask(core, partners[k]))
 
-    def at_load(k):
-        e = k // 4
-        return SY.dma_start(T.ATW[16 * k:16 * k + 16, PAD:PAD + R], T.at[:, R * e:R * e + R])
+    def send_two(rsem, src, dst, left="left"):
+        g.remote_dma_fused([transfer(partners[k], topo.engines(core, partners[k])[k - 1::2], rsem % k, src(k), dst, left)
+                            for k in (1, 2)], local_sem=T.sem[left])
 
-    d_lim = ev(SY.dma_start(T.limi[0:2, :], T.lim[0:1, :]), 16)
-    d_a0 = ev(S.dma_start(T.a0[:, :], T.at[0:1, :]), 16)
+    def iota(out, pattern, base=0, cm=0):
+        return g.iota(out, pattern, base, cm, allow_small_or_imprecise_dtypes=True)
+
+    def select(out, in_, pattern, op, fill, base, cm=-1, s=None):
+        return ev(g.affine_select(out, in_, pattern, op, fill, base, cm), 1, s)
+
     d_fk = ev(S.dma_start(T.fkt[:, :], T.fk[:, :]), 16)
-    d_me = ev(SY.dma_start(T.mei[:, 0:16], T.me[0:1, 0:2048]), 16)
-    ev(SY.dma_start(T.mei[:, 16:32], T.me[0:1, 2048:4096]), 16, d_me)
+    d_lim = ev(SY.dma_start(T.limi[0:1, :], T.lim[0:1, :]), 16)
+    d_a0 = ev(SY.dma_start(T.a0[0:64, :], T.at[0:1, :]), 16)
+    d_me = ev(SY.dma_start(T.mei[:, :], T.me[0:1, :]), 16)
+
+    n = (R - PG) // 2
+    zs = ev(V.memset(T.pw[:, 0:512], 0.0))
+    z0 = ev(V.memset(T.pw[:, 512:1024], 0.0))
+    zb = T.zb[:, :]
+    m_one = ev(V.memset(T.onesb[:, :], 1.0))
+    z_w1 = ev(V.memset(zb, 0.0))
+    z1 = ev(V.memset(T.pw[:, 1024:PU], 0.0))
+    wait("y", zs, z0)
+    wait("s", zs)
+    z2, z3 = new(), new()
+    for k in range(2):
+        ev(SY.dma_start(T.pw[1:128:2, PG + n * k:PG + n * k + n], T.pw[1:128:2, 0:n]), 16, z3)
+    for step in (4, 8, 16):
+        ev(SY.dma_start(T.pw[step // 2:128:step, PG:R], T.pw[1:512 // step:2, 0:n]), 16, z3)
     d_at = new()
-    for k in range(EARLY):
-        ev(at_load(k), 16, d_at)
 
-    z0 = ev(V.memset(T.pw[:, 0:1024], 0.0))
-    m_one = ev(V.memset(T.onesf[:, :], 1.0))
-    ev(V.memset(T.onesb[:, :], 1.0), 1, m_one)
-    m_z = ev(V.memset(T.zb[:, :], 0.0))
-    ev(V.memset(T.Qhi[:, :], 0.0), 1, m_z)
-    z1 = ev(V.memset(T.pw[:, 1024:P1], 0.0))
-    wait("s", z0)
-    z2 = new()
-    for k in range(P2, R, 1024):
-        n = min(1024, R - k)
+    def bulk(lo, hi):
+        for k in range(lo, hi):
+            ev(SY.dma_start(T.ATW[16 * k:16 * k + 16, PAD:PAD + R], T.at[:, R * (k // 4):R * (k // 4) + R]), 16, d_at)
+
+    bulk(0, BULK[0])
+    for k in range(PV, PS, 512):
+        n = min(512, PS - k)
         ev(S.activation(T.pw[:, k:k + n], T.pw[:, 0:n], AF.Copy), 1, z2)
-
+    z4 = ev(iota(T.pw[:, PS:PG], [[0, PG - PS]]))
     c_io = ev(g.iota(T.kc[:, :], [[0, 1]], 0, 1))
-    ev(g.iota(T.rowj[:, :], [[1, 2], [32, 16]], C, 0, allow_small_or_imprecise_dtypes=True), 1, c_io)
-    wait("g", m_one)
-    c_lim = ev(g.affine_select(T.limsel[0:2, :], T.onesf[0:2, :], [[1, 2], [0, 64]], A.is_equal, 0.0, 0, -1))
-    c_q = new()
-    for h in range(2):
-        ev(g.affine_select(T.Qlo[:, 128 * h:128 * h + 128], T.onesb[:, :], [[2, 8], [16, 16]],
-                           A.is_equal, 0.0, h, -1), 1, c_q)
 
-    wait("v", d_lim)
-    v_lim = ev(V.tensor_copy(T.limf[0:2, :], T.limi[0:2, :]))
-    wait("p", v_lim, c_lim)
-    p_lim = ev(PE.matmul(T.b2[:, 480:482], T.limsel[0:2, :], T.limf[0:2, :], True, True))
-    wait("v", d_a0, p_lim)
-    v_cl = ev(V.tensor_scalar(out=T.b2[:, 128:256], in0=T.a0[:, :], scalar1=T.b2[:, 480:481],
-                              scalar2=T.b2[:, 481:482], op0=A.max, op1=A.min))
+    def keys(r, out, e, blocks=range(4)):
+        for a in blocks:
+            ev(V.tensor_copy(out[32 * a:32 * a + 32, 64 * r:64 * r + 64],
+                             T.fkt[32 * r:32 * r + 32, 64 * a:64 * a + 64]), 1, e)
+        return e
+
+    wait("g", d_lim)
+    c_lim = ev(g.partition_broadcast(T.limb[:, :], T.limi[0:1, :], 128))
+    c_j = ev(iota(T.rowj[:, :], [[4, 2], [128, 16]], 4 * C))
+    k0, k1 = new(), new()
+    wait("v", d_fk)
+    keys(order[0], T.KS, k0)
+    wait("v", c_lim)
+    v_lim = new()
+    for e in range(2):
+        ev(V.tensor_copy(T.limf[32 * e:32 * e + 32, :], T.limb[32 * e:32 * e + 32, 2 * e:2 * e + 2]), 1, v_lim)
+    keys(order[1], T.KS, k1, (0, 1))
+    wait("v", d_a0, v_lim)
+    v_cl = ev(V.tensor_scalar(out=T.b2[0:64, 0:256], in0=T.a0[0:64, :], scalar1=T.limf[0:64, 0:1],
+                              scalar2=T.limf[0:64, 1:2], op0=A.max, op1=A.min))
+    keys(order[1], T.KS, k1, (2, 3))
     wait("v", v_cl)
-    v_ps = ev(V.tensor_tensor(T.ps[:, :], T.b2[:, 128:256], T.a0[:, :], A.is_equal))
-    wait("g", v_ps)
-    send_all("h1", lambda r: T.ps[:, :], T.PD[q])
-    ev(V.memset(T.pw[:, P1:P2], 0.0), 1, z1)
-    wait("y", v_ps, z0, z1, z2)
-    d_pw = ev(SY.dma_start(T.pw[32 * q:32 * q + 32:16, :], T.ps[:, :]), 16)
-    wait("y", "h1")
-    for lo, hi in ((0, q), (q + 1, NR)):
-        if lo < hi:
-            ev(SY.dma_start(T.pw[32 * lo:32 * hi:16, :], T.PD[lo:hi]), 16, d_pw)
-    for k in range(EARLY, 8):
-        ev(at_load(k), 16, d_at)
-
-    wait("g", m_z)
-    c_h0, c_h = new(), new()
-    for h in range(2):
-        ev(g.affine_select(T.Qhi[:, 128 * h:128 * h + 128:2], T.onesb[:, 0:64], [[2, 8], [32, 8]],
-                           A.is_equal, 0.0, h - 128, -1), 1, c_h0)
-    c_idb = ev(g.affine_select(T.idb[:, :], T.onesb[:, :], [[1, 128]], A.is_equal, 0.0, 0, -1))
-    wait("g", c_h0)
-    ev(g.affine_select(T.Qhi[:, 0:256:2], T.Qhi[:, 0:256:2], [[1, 2], [2, 8], [32, 8]],
-                       A.not_equal, 1.0, 16 - 128, -1), 1, c_h)
-    c_m = new()
-    pat = [[1, 8], [8, 16]]
-    ev(g.affine_select(T.mats[:, 0:128], T.zb[:, :], pat, A.is_gt, -1.0, 0, -1), 1, c_m)
-    ev(g.affine_select(T.mats[:, 128:256], T.zb[:, :], pat, A.is_ge, -1.0, 0, -1), 1, c_m)
-    ev(g.affine_select(T.mats[:, 256:384], T.onesb[:, :], pat, A.is_equal, 0.0, 0, -1), 1, c_m)
-    z_w1 = ev(g.iota(T.W1[:, 0:C], [[0, C]], 0, 0, allow_small_or_imprecise_dtypes=True))
-    c_r = ev(g.affine_select(T.R16[0:16, :], T.onesb[0:16, 0:16], [[8, 2], [1, 2], [2, 4]], A.is_equal, 0.0, 0, -1))
-    c_rep = ev(g.affine_select(T.rep[0:16, :], T.onesb[0:16, :], [[0, 8], [1, 16]], A.is_equal, 0.0, 0, -1))
-    wait("g", c_r)
-    c_r = ev(g.affine_select(T.R16[0:16, 0:4], T.R16[0:16, 0:4], [[2, 4]], A.not_equal, 1.0, 8, -1))
-    for lo, w in ((4, 256.0 + PAD), (8, -240.0)):
-        ev(g.affine_select(T.R16[0:16, lo:lo + 4], T.R16[0:16, lo:lo + 4], [[0, 4]], A.not_equal, w, 15, -1), 1, c_rep)
-    c_s1 = ev(g.affine_select(T.sele[:, :], T.onesf[:, 0:64], [[16, 2], [1, 16], [32, 2]], A.is_equal, 0.0, 0, -1))
-    wait("g", c_r)
-    ev(g.affine_select(T.R16[0:16, 0:4], T.R16[0:16, 0:4], [[0, 4]], A.not_equal, (256.0 + PAD) / 16, 15, -1), 1, c_rep)
-    wait("g", c_s1)
-    c_sel = ev(g.affine_select(T.sele[:, :], T.sele[:, :], [[16, 2], [1, 16], [32, 2]], A.not_equal, 1.0, 64, -1))
-
-    wait("v", d_fk, c_io)
-    v_off = ev(V.tensor_copy(T.off16[:, :], T.fkt[:, :]))
-    v_k = ev(V.tensor_scalar(out=T.ke[:, :], in0=T.kc[:, :], scalar1=16, scalar2=None, op0=A.bitwise_and))
-    v_ku = ev(V.tensor_scalar(out=T.ku[:, :], in0=T.kc[:, :], scalar1=3, scalar2=None, op0=A.arith_shift_right))
-    v_k2 = ev(V.tensor_scalar(out=T.fhi[:, :], in0=T.fkt[:, :], scalar1=0x1E00, scalar2=None, op0=A.bitwise_and))
-    wait("v", v_k)
-    ev(V.tensor_scalar(out=T.kef[:, :], in0=T.ke[:, :], scalar1=15.0 / 256, scalar2=1.0 / 16, op0=A.mult, op1=A.add),
-       1, v_k2)
-    ev(V.tensor_scalar(out=T.flo[:, :], in0=T.fkt[:, :], scalar1=511, scalar2=None, op0=A.bitwise_and), 1, v_k2)
-    wait("v", v_k2)
-    v_kb = ev(V.tensor_scalar(out=T.fhib[:, :], in0=T.fhi[:, :], scalar1=T.kef[:, :], scalar2=None, op0=A.mult))
-    ev(V.tensor_scalar(out=T.flob[:, :], in0=T.flo[:, :], scalar1=-256.0, scalar2=T.kef[:, :], op0=A.add, op1=A.mult),
-       1, v_kb)
-
-    m_w = ev(V.memset(T.ATW[:, 0:PAD], 0))
-    m_mel = ev(V.memset(T.MEL[:, :], 0.0))
-    wait("v", d_me)
+    v_ps = ev(V.tensor_tensor(T.ps[0:64, :], T.b2[0:64, 0:256], T.a0[0:64, :], A.is_equal))
+    ev(V.memset(T.pw[:, PU:PV], 0.0), 1, z1)
+    keys(order[2], T.KS, k1)
+    wait("v", c_io, d_me)
     v_mp = ev(V.tensor_scalar(out=T.mep[:, 0:32], in0=T.mei[:, :], scalar1=14, scalar2=None, op0=A.arith_shift_right))
     ev(V.tensor_scalar(out=T.mep[:, 32:64], in0=T.mei[:, :], scalar1=0x3F80, scalar2=None, op0=A.bitwise_and), 1, v_mp)
     ev(V.tensor_scalar(out=T.mep[:, 64:96], in0=T.mei[:, :], scalar1=127, scalar2=None, op0=A.bitwise_and), 1, v_mp)
-    wait("v", m_mel)
-    v_mel = ev(V.memset(T.MEL[:, 15:512:16], 1.0))
+    v_k = new()
+    for x, m in enumerate((16, 0x78)):
+        ev(V.tensor_scalar(out=T.kb[:, x:x + 1], in0=T.kc[:, :], scalar1=m, scalar2=None, op0=A.bitwise_and), 1, v_k)
     wait("v", v_mp)
-    for x in range(3):
-        for h in range(2):
-            ev(V.tensor_scalar(out=T.MEL[:, 256 * h + 9 + 2 * x:256 * h + 256:16],
-                               in0=T.mep[:, 32 * x + h:32 * x + 32:2],
-                               scalar1=16384.0 if x == 0 else 1.0, scalar2=None, op0=A.mult), 1, v_mel)
-    wait("v", v_ku)
-    v_kf = ev(V.tensor_scalar(out=T.kuf[:, :], in0=T.ku[:, :], scalar1=2.0, scalar2=None, op0=A.mult))
-    wait("p", v_kb, c_q, c_h, v_mel, c_idb)
-    p_r = new()
+    v_mb = ev(V.tensor_copy(T.meb[:, :], T.mep[:, :]))
+    d_pw = new()
+    wait("y", v_ps, z1, z2, z4)
+    for a in range(4):
+        ev(SY.dma_start(T.pw[32 * a:32 * a + 32:16, :], T.ps[0:64, :]), 16, d_pw)
+    wait("g", k0)
+    send(0, "h0_0", T.KS[:, 64 * order[0]:64 * order[0] + 64], T.KR[:, 64 * q:64 * q + 64])
+    wait("g", m_one)
+    c_4 = select(T.sel4[:, :], T.onesb[:, 0:4], [[32, 4]], A.is_equal, 0.0, 0)
+    c_h0 = select(T.Qhi[:, 0:256:2], T.onesb[:, :], [[1, 2], [2, 8], [32, 8]], A.is_equal, 0.0, -128)
+    wait("g", k1)
+    send_two("h0_%d", lambda k: T.KS[:, 64 * order[k]:64 * order[k] + 64], T.KR[:, 64 * q:64 * q + 64], "gone")
+    wait("y", "gone")
+    bulk(BULK[0], BULK[1])
+
+    wait("g", m_one)
+    wait("g", c_4, c_h0)
+    c_h = select(T.Qhi[:, 0:256:2], T.Qhi[:, 0:256:2], [[1, 2], [2, 8], [32, 8]], A.not_equal, 1.0, 16 - 128)
+    c_4 = select(T.sel4[:, :], T.sel4[:, :], [[32, 4]], A.not_equal, 1.0, 16)
+    c_idb = select(T.idb[:, :], T.onesb[:, :], [[1, 128]], A.is_equal, 0.0, 0)
+    c_q = new()
     for h in range(2):
-        o = T.b0[:, 256 * h:256 * h + 256]
-        PE.matmul(o, T.Qlo[:, 128 * h:128 * h + 128], T.flob[:, :], True, False)
-        PE.matmul(o, T.Qhi[:, 128 * h:128 * h + 128], T.fhib[:, :], False, False)
-        for x in range(2 * h, 2 * h + 2):
-            last = PE.matmul(T.b0[:, 128 * x:128 * x + 128], T.MEL[:, 128 * x:128 * x + 128], T.idb[:, :],
-                             False, x % 2 == 1)
-        ev(last, 1, p_r)
+        select(T.Qlo[:, 128 * h:128 * h + 128], T.onesb[:, :], [[2, 8], [16, 16]], A.is_equal, 0.0, h, s=c_q)
+    pat = [[1, 8], [8, 16]]
+    c_m = select(T.mats[:, 256:384], T.onesb[:, :], pat, A.is_equal, 0.0, 0)
+    wait("g", z_w1)
+    select(T.mats[:, 0:128], zb, pat, A.is_gt, -1.0, 0, s=c_m)
+    select(T.mats[:, 128:256], zb, pat, A.is_ge, -1.0, 0, s=c_m)
 
-    wait("v", d_pw, v_off, z0, z1)
-    wait("s", d_pw, v_off, z0, z1)
-    p_c = new()
-    for lo, hi in ((0, 3), (3, 5), (5, 7), (7, 8)):
-        got = [ev(V.tensor_copy(T.Pg[:, 256 * lo:256 * hi], T.pw[:, :].indirect(T.off16[:, 16 * lo:16 * hi]))),
-               ev(S.activation(T.Pg[:, 2048 + 256 * lo:2048 + 256 * hi],
-                               T.pw[:, :].indirect(T.off16[:, 128 + 16 * lo:128 + 16 * hi]), AF.Copy))]
-        for b in range(2):
-            wait("p", got[b])
-            for uh in range(8 * b + lo, 8 * b + hi):
-                for h in range(2):
-                    w = 16 * h + uh
-                    ev(PE.matmul(T.b2[:, w:w + 1], T.Pg[:, 256 * uh + h:256 * uh + 256:2], T.onesb[:, 0:1], True, True),
-                       1, p_c)
-    wait("s", p_r)
-    s_k1 = ev(S.activation(T.K1[:, :], T.b0[:, :], AF.Copy))
+    wait("s", z_w1, m_one)
+    m_mel = new()
+    for k in range(2):
+        ev(S.activation(T.MEL[:, 16 * k:16 * k + 16, 0:8], zb, AF.Copy), 1, m_mel)
+    ev(S.activation(T.Qhi[:, 1:256:2], zb, AF.Copy), 1, m_mel)
+    s_mel = ev(S.activation(T.MEL[:, :, 15], T.onesb[:, 0:32], AF.Copy))
+    ev(S.activation(T.MEL[:, :, 8:16:2], T.onesb[:, :], AF.Copy, scale=-BIG * 17 / 16), 1, s_mel)
+    wait("v", v_k)
+    v_kf = ev(V.tensor_scalar(out=T.kf[:, 0:1], in0=T.kb[:, 0:1], scalar1=15.0 / 256, scalar2=1.0 / 16, op0=A.mult,
+                              op1=A.add))
+    ev(V.tensor_copy(T.kf[:, 1:2], T.kb[:, 1:2]), 1, v_kf)
+    kef = T.kf[:, 0:1]
+    wait("v", v_kf)
+    v_hi = ev(V.tensor_scalar(out=T.fhib[:, :], in0=T.fkt[:, :], scalar1=BIG - 255.5, scalar2=kef, op0=A.add,
+                              op1=A.mult))
+    v_lo = ev(V.tensor_scalar(out=T.flo[:, :], in0=T.fkt[:, :], scalar1=511, scalar2=None, op0=A.bitwise_and))
+    k_own = keys(q, T.KR, new())
+    wait("v", v_lo, c_j)
+    v_lo = ev(V.tensor_scalar(out=T.flob[:, :], in0=T.flo[:, :], scalar1=-256.0, scalar2=kef, op0=A.add, op1=A.mult))
+    wait("s", v_mb)
+    for h in range(2):
+        for x in range(3):
+            ev(S.activation(T.MEL[:, 16 * h:16 * h + 16, 9 + 2 * x], T.meb[:, 32 * x + h:32 * x + 32:2], AF.Copy,
+                            scale=16384.0 if x == 0 else 1.0), 1, s_mel)
 
-    wait("v", c_m, v_kf)
-    v_h = ev(V.tensor_copy(T.H[:, 0:384], T.mats[:, :]))
-    v_j = ev(V.tensor_scalar(out=T.J[:, :], in0=T.rowj[:, :], scalar1=T.kuf[:, :], scalar2=None, op0=A.add))
-    ev(V.tensor_copy(T.H[:, 512:640], T.onesb[:, :]), 1, v_h)
-    ev(V.tensor_scalar(out=T.H[:, 384:512], in0=T.mats[:, 256:384], scalar1=-1.0, scalar2=None, op0=A.mult), 1, v_h)
-    L1, L1B, IP, NIP, ONE = [T.H[:, 128 * k:128 * k + 128] for k in range(5)]
-    wait("p", v_h, v_j)
-    PE.matmul(T.b3[:, 0:32], IP, T.J[:, :], True, False)
-    wait("v", p_c)
-    v_m = ev(V.tensor_scalar(out=T.Msk[:, :], in0=T.b2[:, 0:32], scalar1=7.5, scalar2=None, op0=A.is_gt))
-    wait("v", v_m)
+    KB = (T.b0, T.b7)
+
+    def high(h):
+        wait("p", v_hi, c_h, m_mel)
+        PE.matmul(KB[h][:, 0:256], T.Qhi[:, 128 * h:128 * h + 128], T.fhib[:, :], True, False)
+
+    def measure(h):
+        wait("p", s_mel, c_idb)
+        for x in range(2):
+            PE.matmul(KB[h][:, x:256:2], T.MEL[:, 16 * h + 8 * x:16 * h + 8 * x + 8, :], T.idb[:, :], False, False)
+
+    def low(h):
+        wait("p", v_lo, c_q)
+        return ev(PE.matmul(KB[h][:, 0:256], T.Qlo[:, 128 * h:128 * h + 128], T.flob[:, :], False, True))
+
+    turn = order + [q]
+    CB = [T.b1, T.b2, T.b4, T.b5]
+    wait("v", d_pw, z3)
+    wait("s", d_pw, z3)
+    wait("p", c_4, v_ps)
+    high(0)
+    done = [new() for n in range(4)]
+
+    def evacuate(k):
+        wait("v", done[k])
+        wait("g", ev(V.tensor_copy(T.CS[:, 32 * k:32 * k + 32], CB[k][:, 0:32])))
+        send(k, "h1_%d" % k, T.CS[:, 32 * k:32 * k + 32], T.CR[:, 32 * k:32 * k + 32])
+
+    for n in range(4):
+        r = turn[n]
+        got = []
+        for k, runs in zip("vs", ROUNDS[n]):
+            wait(k, "h0_%d" % n if n < 3 else k_own)
+            for x, (lo, hi) in enumerate(runs):
+                out = T.Pg[:, 1024 * n + 16 * lo:1024 * n + 16 * hi]
+                win = T.pw[:, :].indirect(T.KR[:, 64 * r + lo:64 * r + hi])
+                got.append((lo, hi, ev(V.tensor_copy(out, win) if k == "v" else S.activation(out, win, AF.Copy))))
+                if k == "v" and n and x == (0 if n == 3 else len(runs) - 1):
+                    evacuate(n - 1)
+        for u in BLOCKS:
+            wait("p", *[e for lo, hi, e in got if lo < 16 * u + 16 and hi > 16 * u])
+            for h in range(2):
+                ev(PE.matmul(CB[n][:, 16 * h + u:16 * h + 16:4],
+                             T.Pg[:, 1024 * n + 256 * u + h:1024 * n + 256 * u + 256:2], T.sel4[:, :], True, True),
+                   1, done[n])
+        if n == 0:
+            high(1)
+        if n == 1:
+            measure(0)
+        if n == 2:
+            measure(1)
+            p_k = [low(h) for h in range(2)]
+    g.sem_inc(T.sem.issued, 1)
+    total["issued"] = 1
+    wait("y", "issued", *[e for lo, hi, e in got])
+    z_w2 = ev(SY.dma_start(T.pw[0:128:16, 0:C], T.pw[1:128:16, 0:C]), 16)
+    bulk(BULK[1], 8)
+    s_k1 = new()
+    for h in range(2):
+        wait("s", p_k[h])
+        ev(S.activation(T.K1[:, 256 * h:256 * h + 256], KB[h][:, 0:256], AF.Copy), 1, s_k1)
+    wait("v", "h1_0", "h1_1")
+    t = ev(V.tensor_tensor(T.thr[:, 0:32], T.CR[:, 0:32], T.CR[:, 32:64], A.add))
+    v_j = ev(V.tensor_scalar(out=T.J[:, 0:32], in0=T.rowj[:, :], scalar1=T.kf[:, 1:2], scalar2=0.25, op0=A.add,
+                             op1=A.mult))
+    ev(V.tensor_scalar(out=T.J[:, 32:64], in0=T.rowj[:, :], scalar1=T.kf[:, 1:2], scalar2=-0.25, op0=A.add,
+                       op1=A.mult), 1, v_j)
+    wait("v", t)
+    t = ev(V.tensor_scalar(out=T.thr[:, 32:64], in0=T.thr[:, 0:32], scalar1=-1.0, scalar2=7.5, op0=A.mult, op1=A.add))
+    m_w = ev(V.memset(T.ATW[:, 0:PAD], 0))
+    wait("v", t, done[3])
+    t = ev(V.tensor_tensor(T.thr[:, 64:96], T.thr[:, 32:64], CB[3][:, 0:32], A.subtract))
+    L1, L1B, IP, ONE = T.mats[:, 0:128], T.mats[:, 128:256], T.mats[:, 256:384], T.onesb[:, :]
+    wait("p", c_m, v_j)
+    PE.matmul(T.b3[:, 0:32], IP, T.J[:, 0:32], True, False)
+
+    c_r = select(T.R16[0:16, :], T.onesb[0:16, 0:16], [[8, 2], [1, 2], [2, 4]], A.is_equal, 0.0, 0)
+    c_rep = select(T.rep[0:16, :], T.onesb[0:16, :], [[0, 8], [1, 16]], A.is_equal, 0.0, 0)
+    wait("g", c_r)
+    c_r = select(T.R16[0:16, 0:4], T.R16[0:16, 0:4], [[2, 4]], A.not_equal, 1.0, 8)
+    for lo, w in ((4, 256.0 + PAD), (8, -240.0)):
+        select(T.R16[0:16, lo:lo + 4], T.R16[0:16, lo:lo + 4], [[0, 4]], A.not_equal, w, 15, s=c_rep)
+    c_s1 = select(T.sele[:, :], T.onesb[:, 0:64], [[16, 2], [1, 16], [32, 2]], A.is_equal, 0.0, 0)
+    wait("g", c_r)
+    select(T.R16[0:16, 0:4], T.R16[0:16, 0:4], [[0, 4]], A.not_equal, (256.0 + PAD) / 16, 15, s=c_rep)
+    wait("g", c_s1)
+    c_sel = select(T.sele[:, :], T.sele[:, :], [[16, 2], [1, 16], [32, 2]], A.not_equal, 1.0, 64)
+
+    wait("v", t, "h1_2")
+    v_m = ev(V.tensor_tensor(T.Msk[:, :], T.CR[:, 64:96], T.thr[:, 64:96], A.is_gt))
+    wait("v", v_m, v_j)
     v_sc = ev(V.tensor_tensor_scan(T.Sc[:, :], T.Msk[:, 0:16], T.Msk[:, 16:32], 0.0, A.add, A.add))
-    v_mj = ev(V.tensor_tensor(T.MJ[:, :], T.Msk[:, :], T.J[:, :], A.mult))
+    v_mj = ev(V.tensor_tensor(T.MJ[:, :], T.Msk[:, :], T.J[:, 32:64], A.mult))
     wait("p", v_m)
     PE.matmul(T.b3[:, 0:32], L1, T.Msk[:, :], False, False)
     PE.matmul(T.b3[:, 0:16], L1, T.Msk[:, 16:32], False, False)
@@ -260,33 +331,36 @@ def rank_program(g, core, T, topo):
     PE.matmul(T.b3[:, 0:16], ONE, T.Sc[:, :], False, False)
     PE.matmul(T.b3[:, 16:32], ONE, T.Sc[:, :], False, False)
     wait("p", v_mj)
-    p_pos = ev(PE.matmul(T.b3[:, 0:32], NIP, T.MJ[:, :], False, True))
+    p_pos = ev(PE.matmul(T.b3[:, 0:32], IP, T.MJ[:, :], False, True))
+    wait("p", s_k1)
     p_nt = ev(PE.matmul(T.b7[:, 256:257], ONE, T.Sc[:, 15:16], True, True))
     wait("p", c_rep)
     p_rl = ev(PE.matmul(T.b1[:, 0:16], T.rep[0:16, :], T.R16[0:16, :], True, True))
     wait("v", p_pos)
     v_o3 = ev(V.tensor_copy(T.off3[:, :], T.b3[:, 0:32]))
+    wait("s", p_nt)
+    s_nt = ev(S.activation(T.nt[:, :], T.b7[:, 256:257], AF.Copy))
     wait("s", p_rl)
     s_rl = ev(S.activation(T.RL[:, :], T.b1[:, 0:16], AF.Copy))
     s_r1 = ev(S.activation(T.rm3[:, 0:3], T.b1[:, 12:15], AF.Copy, accum_out=T.rm1[:, :]))
-    wait("s", p_nt)
-    s_nt = ev(S.activation(T.nt[:, :], T.b7[:, 256:257], AF.Copy))
     wait("s", s_r1)
     s_rm = ev(S.activation(T.RM[:, :], T.onesb[:, 0:16], AF.Copy, scale=T.rm1[:, :]))
 
-    wait("v", v_o3, s_k1, z_w1)
-    v_w1 = ev(V.tensor_copy(T.W1[:, :].indirect(T.off3[:, :]), T.K1[:, :]))
+    wait("v", v_o3, s_k1, z_w2)
+    v_w1 = ev(V.tensor_copy(T.pw[:, 0:3584].indirect(T.off3[:, :]), T.K1[:, :]))
     wait("p", v_w1, s_rl)
     p_l = new()
     for c in range(6):
         for j1 in range(2):
             y = 4 * (c // 2) + 2 * j1 + c % 2
-            ev(PE.matmul(T.b4[:, y:144:12], T.W1[:, 768 * j1 + c:768 * j1 + 768:6], T.RL[:, 0:12], True, True), 1, p_l)
+            ev(PE.matmul(T.b4[:, y:144:12], T.pw[:, 768 * j1 + c:768 * j1 + 768:6], T.RL[:, 0:12], True, True), 1, p_l)
     wait("s", v_w1)
-    s_w2 = new()
+    wait("v", v_w1)
+    s_w2 = [new() for ch in range(3)]
     for c in range(6):
         for jb in range(4):
-            ev(S.activation(T.W2[:, c // 2, :, jb, c % 2, :], T.W1[:, 384 * jb + c:384 * jb + 384:6], AF.Copy), 1, s_w2)
+            out, in_ = T.W2[:, c // 2, :, jb, c % 2, :], T.pw[:, 384 * jb + c:384 * jb + 384:6]
+            ev(V.tensor_copy(out, in_) if 4 * c + jb < WV else S.activation(out, in_, AF.Copy), 1, s_w2[c // 2])
     wait("v", p_l)
     v_z = ev(V.tensor_scalar(out=T.Z[:, :], in0=T.b4[:, 96:144], scalar1=ROUND, scalar2=ROUND, op0=A.add,
                              op1=A.subtract))
@@ -300,68 +374,66 @@ def rank_program(g, core, T, topo):
             ev(V.tensor_scalar(out=T.Ls[64 * e:64 * e + 64, :, j0, :], in0=T.T2[64 * j0:64 * j0 + 64, 48 * e:48 * e + 48],
                                scalar1=1.0 if e else 16.0, scalar2=None, op0=A.mult), 1, v_lu)
     wait("g", v_lu)
-    send_all("h2_%d" % q, lambda r: T.Ls[:, 6 * r:6 * r + 6, :, :], T.Lr[:, 24 * q:24 * q + 24])
+    send(0, "h2_0", T.Ls[:, 6 * order[0]:6 * order[0] + 6, :, :], T.Lr[:, 24 * q:24 * q + 24])
+    send_two("h2_%d", lambda k: T.Ls[:, 6 * order[k]:6 * order[k] + 6, :, :], T.Lr[:, 24 * q:24 * q + 24])
     wait("g", s_nt)
     ev(g.dma_start(T.y[:, C:C + 1], T.nt[0:16, :], allow_slow_non_contiguous=True), 16)
 
+    wait("p", s_rm)
+    for ch in range(3):
+        wait("p", s_w2[ch])
+        for a in range(4):
+            c0 = 64 * ch + 32 * (a % 2) + a // 2
+            PE.matmul(T.b5[:, c0:c0 + 31:2], T.W2[:, ch, a, :, :, :], T.RM[:, :], ch + a == 0, False)
     wait("v", v_lu)
     v_own = ev(V.tensor_copy(T.Lr[:, 24 * q:24 * q + 24], T.Ls[:, 6 * q:6 * q + 6, :, :]))
     wait("v", v_own, d_at, m_w)
-    wait("p", c_sel, s_rm, s_nt, s_k1)
-    SB, LB = [T.S0, T.S1, T.S2], [T.L0, T.L1, T.L2]
+    wait("p", c_sel, s_nt, s_k1, s_rl, s_r1)
 
-    def gather(r, lo, hi, out):
+    def gather(r, lo, hi, out, done=None):
         e = ev(V.tensor_copy(T.G[:, 384 * r + 128 * lo:384 * r + 128 * hi],
                              T.ATW[:, :].indirect(T.Lr[:, 24 * r + 8 * lo:24 * r + 8 * hi])))
         wait("p", e)
-        done = new()
+        done = done or new()
         for ch in range(lo, hi):
-            last = PE.matmul(out[:, 64 * ch:64 * ch + 64], T.G[:, 384 * r + 128 * ch:384 * r + 128 * ch + 128],
-                             T.sele[:, :], True, r != q)
-            if r == q:
-                wait("p", s_w2)
-                for a in range(4):
-                    c0 = 64 * ch + 32 * (a % 2) + a // 2
-                    last = PE.matmul(out[:, c0:c0 + 31:2], T.W2[:, ch, a, :, :, :], T.RM[:, :],
-                                     False, a == 3)
-            ev(last, 1, done)
+            i = PE.matmul(out[:, 64 * ch:64 * ch + 64], T.G[:, 384 * r + 128 * ch:384 * r + 128 * ch + 128],
+                          T.sele[:, :], r != q, r != q or ch == 2)
+            if r != q or ch == 2:
+                ev(i, 1, done)
         return done
 
-    p_own = gather(q, 0, 3, T.b5)
-    for k in range(2):
-        r = order[k]
-        wait("v", "h2_%d" % r)
-        s = new()
-        for lo, hi, b in (((0, 3, T.b3),), ((0, 2, T.b7), (2, 3, T.b2)))[k]:
-            wait("s", gather(r, lo, hi, b))
-            ev(S.activation(SB[k][:, 64 * lo:64 * hi], b[:, 64 * lo:64 * hi], AF.Copy), 1, s)
-        wait("g", s)
-        g.remote_dma_fused([transfer(partners[k], topo.engines(core, partners[k]), "h3_%d" % k, SB[k][:, :],
-                                     LB[k][:, :])], local_sem=T.sem.left)
-    r = order[2]
-    wait("v", "h2_%d" % r)
-    pa = gather(r, 0, 2, T.b0)
-    wait("p", s_rl, s_r1)
-    pb = gather(r, 2, 3, T.b1)
-    wait("v", pa)
-    v_tr = ev(V.transpose(T.S2[:, 0:128], T.b0[:, 0:128]))
-    wait("v", pb)
-    ev(V.transpose(T.S2[:, 128:192], T.b1[:, 128:192]), 1, v_tr)
-    wait("g", v_tr)
-    g.remote_dma_fused([transfer(partners[2], topo.engines(core, partners[2]), "h3_2", T.S2[:, :], T.L2[:, :, :, :])],
-                       local_sem=T.sem.left)
+    gather(q, 0, 1, T.b5)
+    p_own = gather(q, 1, 3, T.b5)
+    wait("v", "h2_0")
+    s = []
+    for lo, hi, b in ((0, 1, T.b3), (1, 2, T.b7), (2, 3, T.b2)):
+        wait("s", gather(order[0], lo, hi, b))
+        s.append(ev(S.activation(T.S0[:, 64 * lo:64 * hi], b[:, 64 * lo:64 * hi], AF.Copy)))
+    wait("g", *s)
+    send(0, "h3_0", T.S0[:, :], T.L0[:, :])
+    wait("v", "h2_1")
+    p1 = gather(order[1], 1, 3, T.b1, gather(order[1], 0, 1, T.b1))
+    wait("v", "h2_2")
+    pa = gather(order[2], 0, 2, T.b0)
+    pb = gather(order[2], 2, 3, T.b4)
+    for p, rsem, k, out, bank, dst, lo, hi in ((p1, "h3_1", 1, T.S1, T.b1, T.L1[:, :], 0, 192),
+                                               (pa, "h3_2", 2, T.S2, T.b0, T.L2[:, 0:4, :, :], 0, 128),
+                                               (pb, "h3_3", 2, T.S2, T.b4, T.L2[:, 4:6, :, :], 128, 192)):
+        wait("v", p)
+        wait("g", ev(V.transpose(out[:, lo:hi], bank[:, lo:hi])))
+        send(k, rsem, out[:, lo:hi], dst)
 
     acc = T.b5[:, 0:192]
-    a = p_own
-    for k in range(2):
-        wait("v", a, "h3_%d" % k)
-        a = ev(V.tensor_tensor(acc, acc, LB[k][:, :], A.add))
+    wait("v", p_own, "h3_0")
+    a = ev(V.tensor_tensor(acc, acc, T.L0[:, :], A.add))
     wait("v", a)
-    t = ev(V.transpose(T.bT[:, 0:6, :, :], acc))
-    wait("v", t, "h3_2")
+    a = ev(V.transpose(T.bT[:, 0:6, :, :], acc))
+    wait("v", a, "h3_1")
+    a = ev(V.tensor_tensor(T.bT[:, 0:6, :, :], T.bT[:, 0:6, :, :], T.L1[:, :], A.add))
     x = new()
     for c in range(6):
         ch, xl = c // 2, c % 2
+        wait("v", a, "h3_3" if ch == 2 else "h3_2")
         ev(V.tensor_tensor(T.O[:, c:192:6], T.bT[:, 2 * ch:2 * ch + 2, xl, :], T.L2[:, 2 * ch:2 * ch + 2, xl, :], A.add),
            1, x)
     for n, jbs in (("y", (0, 1)), ("s", (2, 3))):

@@ -2,28 +2,41 @@ from concourse.bass import DstId, RemoteDMATransfer
 from concourse.mybir import AluOpType as A, ActivationFunctionType as AF
 
 R, F, C, D, NR = 8192, 4096, 1536, 2, 4
-PU, PV, PS, PG = 2304, 3072, 5632, 6144
-BULK = (1, 4)
+PU, PV, PS, PG = 2304, 3200, 5888, 5888
+RS, RG, RV = 704, 0, 128
+RS1 = 320
+NP = (3, 1)
+BE, BQ = 4096, 4608
+CX, B1, B3 = R, R, 0
+GORD = ("", "", "i2j", "mrs", "1")
+LATE = False
+SPLIT = ((((0, 12),), ((12, 24),)), (((0, 8), (16, 20)), ((8, 16), (20, 24))), (((0, 8),), ((8, 16), (16, 24))))
+CH = ((0, 1, 2), (0, 1, 2))
+TWO = True
+OWNF = 12
+RAW1 = False
+PWQ = "yy"
 PAD = 8
 BIG = 1.5 * 2.0 ** 16
 ROUND = 1.5 * 2.0 ** 32
-ROUNDS = ((((0, 32),), ((32, 64),)), (((0, 32),), ((32, 64),)), (((0, 16), (16, 32)), ((48, 64), (32, 48))),
-          (((0, 8), (8, 30)), ((48, 64), (30, 48))))
+ROUNDS = ((((0, 30),), ((30, 64),)), (((0, 30),), ((30, 64),)), (((0, 16), (16, 32)), ((48, 64), (32, 48))),
+          (((0, 24),), ((48, 64), (24, 48))))
 BLOCKS = (3, 0, 2, 1)
-WV = 10
+WV = 6
 
 SCRATCH = {
-    "limi": ("sbuf", [128, 4], "int32"), "limb": ("sbuf", [128, 4], "int32"), "limf": ("sbuf", [128, 2], "float32"),
+    "limi": ("sbuf", [128, 4], "int32"), "limf": ("sbuf", [128, 4], "float32"), "onesf": ("sbuf", [128, 32], "float32"),
+    "X1": ("sbuf", [128, 128], "bfloat16"), "X2": ("sbuf", [128, 128], "bfloat16"),
     "a0": ("sbuf", [128, 256], "int32"), "ps": ("sbuf", [128, 256], "bfloat16"),
     "pw": ("sbuf", [128, R], "bfloat16"), "Pg": ("sbuf", [128, F], "bfloat16"),
-    "kc": ("sbuf", [128, 1], "int32"), "kb": ("sbuf", [128, 2], "int32"), "kf": ("sbuf", [128, 2], "float32"),
+    "kc": ("sbuf", [128, 1], "int32"), "kb": ("sbuf", [128, 4], "int32"), "kf": ("sbuf", [128, 4], "bfloat16"),
     "fkt": ("sbuf", [128, 256], "int32"),
-    "KS": ("sbuf", [128, 256], "uint16"), "KR": ("sbuf", [128, 256], "uint16"),
+    "KS": ("sbuf", [128, 192], "uint16"), "KR": ("sbuf", [128, 256], "uint16"),
     "sel4": ("sbuf", [128, 4], "bfloat16"),
-    "CS": ("sbuf", [128, 96], "bfloat16"), "CR": ("sbuf", [128, 96], "bfloat16"), "thr": ("sbuf", [128, 96], "float32"),
-    "fhi": ("sbuf", [128, 256], "int32"), "flo": ("sbuf", [128, 256], "int32"),
+    "CS": ("sbuf", [128, 96], "bfloat16"), "CR": ("sbuf", [128, 96], "bfloat16"),
+    "flo": ("sbuf", [128, 256], "int32"),
     "fhib": ("sbuf", [128, 256], "bfloat16"), "flob": ("sbuf", [128, 256], "bfloat16"),
-    "K1": ("sbuf", [128, 512], "bfloat16"), "zb": ("sbuf", [128, 128], "bfloat16"),
+    "K1": ("sbuf", [128, 512], "bfloat16"),
     "W2": ("sbuf", [128, 3, 4, 4, 2, 16], "bfloat16"),
     "mei": ("sbuf", [128, 32], "int32"), "mep": ("sbuf", [128, 96], "int32"), "meb": ("sbuf", [128, 96], "bfloat16"),
     "MEL": ("sbuf", [128, 32, 16], "bfloat16"),
@@ -36,19 +49,20 @@ SCRATCH = {
     "rm3": ("sbuf", [128, 4], "float32"), "rm1": ("sbuf", [128, 1], "float32"),
     "Msk": ("sbuf", [128, 32], "float16"), "Sc": ("sbuf", [128, 16], "float16"),
     "MJ": ("sbuf", [128, 32], "float16"), "off3": ("sbuf", [128, 32], "uint16"),
+    "Rm": ("sbuf", [128, 128], "float32"),
     "nt": ("sbuf", [128, 1], "float32"),
     "Z": ("sbuf", [128, 48], "float32"), "T2": ("sbuf", [128, 96], "float32"),
     "Ls": ("sbuf", [128, 24, 2, 2], "uint16"), "Lr": ("sbuf", [128, NR * 24], "uint16"),
-    "ATW": ("sbuf", [128, R + PAD], "int32"), "G": ("sbuf", [128, C], "float32"),
-    "S0": ("sbuf", [128, 192], "float32"), "S1": ("sbuf", [128, 192], "float32"), "S2": ("sbuf", [128, 192], "float32"),
-    "L0": ("sbuf", [128, 192], "float32"), "L1": ("sbuf", [128, 192], "float32"),
+    "ATW": ("sbuf", [128, R + PAD], "float32"), "G": ("sbuf", [128, C], "float32"),
+    "S1": ("sbuf", [128, 192], "float32"), "S2": ("sbuf", [128, 192], "float32"),
+    "L0": ("sbuf", [128, 384], "float32"), "L1": ("sbuf", [128, 384], "float32"),
     "L2": ("sbuf", [128, 6, 2, 16], "float32"), "O": ("sbuf", [128, 192], "float32"),
     "bT": ("psum", [128, 16, 2, 16], "float32"),
 }
 for _b in (0, 1, 2, 3, 4, 5, 7):
     SCRATCH["b%d" % _b] = ("psum", [128, 512], "float32")
 NEV = 132
-SEMAPHORES = (["e%d" % _i for _i in range(NEV)] + ["left", "issued", "gone", "sent", "h3_3"]
+SEMAPHORES = (["e%d" % _i for _i in range(NEV)] + ["left", "issued", "gone", "h3_3"]
               + ["h%d_%d" % (_h, _k) for _h in range(4) for _k in range(3)])
 
 
@@ -63,13 +77,14 @@ def rank_program(g, core, T, topo):
     def new():
         s = "e%d" % used[0]
         used[0] += 1
+        total[s] = 0
         return s
 
     def ev(inst, n=1, s=None):
         if s is None:
             s = new()
         inst.then_inc(T.sem[s], n)
-        total[s] = total.get(s, 0) + n
+        total[s] += n
         return s
 
     def wait(k, *names):
@@ -86,9 +101,10 @@ def rank_program(g, core, T, topo):
     partners = [far[at], far[1 - at], mine[1 - at]]
     order = [T.rank_of(c) for c in partners]
     for k in range(3):
-        total["h0_%d" % k] = total["h2_%d" % k] = 8 if k else 16
-        total["h1_%d" % k] = total["h3_%d" % k] = 16
-    total["h3_3"] = 16
+        total["h0_%d" % k] = 8 if k else 16
+        total["h1_%d" % k] = total["h2_%d" % k] = total["h3_%d" % k] = 16
+    if TWO:
+        total["h3_3"] = 16
 
     def transfer(c, engines, rsem, src, dst, left="left"):
         rid, pid, _ = topo.addr(c)
@@ -117,12 +133,12 @@ def rank_program(g, core, T, topo):
     d_me = ev(SY.dma_start(T.mei[:, :], T.me[0:1, :]), 16)
 
     n = (R - PG) // 2
-    zs = ev(V.memset(T.pw[:, 0:512], 0.0))
-    z0 = ev(V.memset(T.pw[:, 512:1024], 0.0))
-    zb = T.zb[:, :]
+    zs = ev(V.memset(T.pw[:, 0:256], 0.0))
+    z0 = ev(V.memset(T.pw[:, 256:n], 0.0))
     m_one = ev(V.memset(T.onesb[:, :], 1.0))
-    z_w1 = ev(V.memset(zb, 0.0))
-    z1 = ev(V.memset(T.pw[:, 1024:PU], 0.0))
+    m_of = ev(V.memset(T.onesf[0:1, :], 1.0))
+    z1 = ev(V.memset(T.pw[:, n:PU], 0.0))
+    c_io = ev(g.iota(T.kc[:, :], [[0, 1]], 0, 1))
     wait("y", zs, z0)
     wait("s", zs)
     z2, z3 = new(), new()
@@ -130,199 +146,258 @@ def rank_program(g, core, T, topo):
         ev(SY.dma_start(T.pw[1:128:2, PG + n * k:PG + n * k + n], T.pw[1:128:2, 0:n]), 16, z3)
     for step in (4, 8, 16):
         ev(SY.dma_start(T.pw[step // 2:128:step, PG:R], T.pw[1:512 // step:2, 0:n]), 16, z3)
-    d_at = new()
 
-    def bulk(lo, hi):
-        for k in range(lo, hi):
-            ev(SY.dma_start(T.ATW[16 * k:16 * k + 16, PAD:PAD + R], T.at[:, R * (k // 4):R * (k // 4) + R]), 16, d_at)
+    XP = 128 * sum(NP)
+    x0 = XP + RS + RG + RV
+    d_at, d_a1, r_at = new(), new(), new()
+    d_c = []
 
-    bulk(0, BULK[0])
-    for k in range(PV, PS, 512):
-        n = min(512, PS - k)
+    def first(e, lo, hi):
+        d_c.append(ev(g.dma_start(T.ATW[64 * e:64 * e + 16, PAD + lo:PAD + hi], T.at[:, R * e + lo:R * e + hi]), 16))
+
+    def bulk(*ks):
+        for k, lo, hi in ks:
+            if lo >= hi:
+                continue
+            wait("y", d_c[2 if k < 4 and hi > CX else k // 4])
+            ev(SY.dma_start(T.ATW[16 * k:16 * k + 16, PAD + lo:PAD + hi],
+                            T.ATW[64 * (k // 4):64 * (k // 4) + 16, PAD + lo:PAD + hi]), 16, d_at if k % 4 > 1 or lo >= x0 else d_a1)
+
+    def repeat(k, lo, hi):
+        wait(k, d_a1, *d_c[:2])
+        for e in range(2):
+            out, in_ = (T.ATW[64 * e + p:64 * e + p + 32, PAD + XP + lo:PAD + XP + hi] for p in (32, 0))
+            ev(S.activation(out, in_, AF.Copy) if k == "s" else V.tensor_copy(out, in_) if k == "v" else
+               g.affine_select(out, in_, [[0, hi - lo]], A.is_ge, 0.0, 0, 0), 1, r_at)
+
+    def spread(bank, lo, n):
+        e = new()
+        wait("p", cs["m"], d_cb, d_c[0])
+        for x in range(n):
+            ev(PE.matmul(bank[:, 128 * x:128 * x + 128], T.Rm[0:32, :],
+
+                         T.ATW[0:32, PAD + lo + 128 * x:PAD + lo + 128 * x + 128], True, True), 1, e)
+        return e
+
+    def put(k, e, bank, lo, n):
+        wait(k, e)
+        out, in_ = T.ATW[:, PAD + lo:PAD + lo + 128 * n], bank[:, 0:128 * n]
+        ev(S.activation(out, in_, AF.Copy) if k == "s" else V.tensor_copy(out, in_), 1, r_at)
+
+    if not LATE:
+        first(0, 0, CX)
+    for k in (PV, PV + 256):
+        ev(S.activation(T.pw[:, k:k + 256], T.pw[:, 0:256], AF.Copy), 1, z2)
+    wait("s", z0)
+    for k in range(PV + 512, PS, 1024):
+        n = min(1024, PS - k)
         ev(S.activation(T.pw[:, k:k + n], T.pw[:, 0:n], AF.Copy), 1, z2)
-    z4 = ev(iota(T.pw[:, PS:PG], [[0, PG - PS]]))
-    c_io = ev(g.iota(T.kc[:, :], [[0, 1]], 0, 1))
+    if PG > PS:
+        ev(iota(T.pw[:, PS:PG], [[0, PG - PS]]), 1, z2)
 
-    def keys(r, out, e, blocks=range(4)):
+    def consts(names):
+        for x in names:
+            if x == "1":
+                cs[x] = ev(iota(T.X1[:, :], [[2, 8], [16, 16]]))
+            if x == "2":
+                cs[x] = ev(iota(T.X2[:, :], [[1, 8], [8, 16]]))
+            if x == "j":
+                cs[x] = ev(iota(T.rowj[:, :], [[4, 2], [128, 16]], 4 * C))
+            if x == "i":
+                wait("g", m_one)
+                cs[x] = select(T.idb[:, :], T.onesb[:, :], [[1, 128]], A.is_equal, 0.0, 0)
+            if x == "m":
+                cs[x] = select(T.Rm[0:32, :], T.onesb[0:32, :], [[16, 2], [0, 4], [1, 16]], A.is_equal, 0.0, 0)
+            if x == "r":
+                c_r = select(T.R16[0:16, :], T.onesb[0:16, 0:16], [[8, 2], [1, 2], [2, 4]], A.is_equal, 0.0, 0)
+                cs[x] = select(T.rep[0:16, :], T.onesb[0:16, :], [[0, 8], [1, 16]], A.is_equal, 0.0, 0)
+                wait("g", c_r)
+                c_r = select(T.R16[0:16, 0:4], T.R16[0:16, 0:4], [[2, 4]], A.not_equal, 1.0, 8)
+                for lo, w in ((4, 256.0 + PAD), (8, -240.0)):
+                    select(T.R16[0:16, lo:lo + 4], T.R16[0:16, lo:lo + 4], [[0, 4]], A.not_equal, w, 15, s=cs[x])
+                wait("g", c_r)
+                select(T.R16[0:16, 0:4], T.R16[0:16, 0:4], [[0, 4]], A.not_equal, (256.0 + PAD) / 16, 15, s=cs[x])
+            if x == "s":
+                wait("g", select(T.sele[:, :], T.onesb[:, 0:64], [[16, 2], [1, 16], [32, 2]], A.is_equal, 0.0, 0))
+                cs[x] = select(T.sele[:, :], T.sele[:, :], [[16, 2], [1, 16], [32, 2]], A.not_equal, 1.0, 64)
+
+    cs = {}
+    consts(GORD[0])
+
+    def keys(r, out, x, e, blocks=range(4)):
         for a in blocks:
-            ev(V.tensor_copy(out[32 * a:32 * a + 32, 64 * r:64 * r + 64],
+            ev(V.tensor_copy(out[32 * a:32 * a + 32, 64 * x:64 * x + 64],
                              T.fkt[32 * r:32 * r + 32, 64 * a:64 * a + 64]), 1, e)
         return e
 
-    wait("g", d_lim)
-    c_lim = ev(g.partition_broadcast(T.limb[:, :], T.limi[0:1, :], 128))
-    c_j = ev(iota(T.rowj[:, :], [[4, 2], [128, 16]], 4 * C))
     k0, k1 = new(), new()
+    wait("v", d_lim)
+    v_lim = ev(V.tensor_copy(T.limf[0:1, :], T.limi[0:1, :]))
     wait("v", d_fk)
-    keys(order[0], T.KS, k0)
-    wait("v", c_lim)
-    v_lim = new()
+    keys(order[0], T.KS, 0, k0)
+    wait("p", v_lim, m_of)
+    p_lim = new()
     for e in range(2):
-        ev(V.tensor_copy(T.limf[32 * e:32 * e + 32, :], T.limb[32 * e:32 * e + 32, 2 * e:2 * e + 2]), 1, v_lim)
-    keys(order[1], T.KS, k1, (0, 1))
-    wait("v", d_a0, v_lim)
-    v_cl = ev(V.tensor_scalar(out=T.b2[0:64, 0:256], in0=T.a0[0:64, :], scalar1=T.limf[0:64, 0:1],
-                              scalar2=T.limf[0:64, 1:2], op0=A.max, op1=A.min))
-    keys(order[1], T.KS, k1, (2, 3))
+        ev(PE.matmul(T.b3[32 * e:32 * e + 32, 0:2], T.onesf[0:1, :], T.limf[0:1, 2 * e:2 * e + 2], True, True), 1, p_lim)
+    wait("v", d_a0, p_lim)
+    v_cl = ev(V.tensor_scalar(out=T.b2[0:64, 0:256], in0=T.a0[0:64, :], scalar1=T.b3[0:64, 0:1],
+                              scalar2=T.b3[0:64, 1:2], op0=A.max, op1=A.min))
+    keys(order[1], T.KS, 1, k1, (0, 1))
     wait("v", v_cl)
     v_ps = ev(V.tensor_tensor(T.ps[0:64, :], T.b2[0:64, 0:256], T.a0[0:64, :], A.is_equal))
     ev(V.memset(T.pw[:, PU:PV], 0.0), 1, z1)
-    keys(order[2], T.KS, k1)
-    wait("v", c_io, d_me)
+    keys(order[1], T.KS, 1, k1, (2, 3))
+    keys(order[2], T.KS, 2, k1)
+    wait("v", d_me, c_io)
     v_mp = ev(V.tensor_scalar(out=T.mep[:, 0:32], in0=T.mei[:, :], scalar1=14, scalar2=None, op0=A.arith_shift_right))
     ev(V.tensor_scalar(out=T.mep[:, 32:64], in0=T.mei[:, :], scalar1=0x3F80, scalar2=None, op0=A.bitwise_and), 1, v_mp)
     ev(V.tensor_scalar(out=T.mep[:, 64:96], in0=T.mei[:, :], scalar1=127, scalar2=None, op0=A.bitwise_and), 1, v_mp)
     v_k = new()
-    for x, m in enumerate((16, 0x78)):
+    for x, m in enumerate((16, 0x78, 0x6F)):
         ev(V.tensor_scalar(out=T.kb[:, x:x + 1], in0=T.kc[:, :], scalar1=m, scalar2=None, op0=A.bitwise_and), 1, v_k)
-    wait("v", v_mp)
+    v_kf = ev(V.tensor_copy(T.kf[:, 3:4], T.kc[:, :]))
+    v_lo = ev(V.tensor_scalar(out=T.flo[:, :], in0=T.fkt[:, :], scalar1=511, scalar2=None, op0=A.bitwise_and))
+    wait("v", v_mp, v_k)
     v_mb = ev(V.tensor_copy(T.meb[:, :], T.mep[:, :]))
-    d_pw = new()
-    wait("y", v_ps, z1, z2, z4)
-    for a in range(4):
-        ev(SY.dma_start(T.pw[32 * a:32 * a + 32:16, :], T.ps[0:64, :]), 16, d_pw)
-    wait("g", k0)
-    send(0, "h0_0", T.KS[:, 64 * order[0]:64 * order[0] + 64], T.KR[:, 64 * q:64 * q + 64])
-    wait("g", m_one)
-    c_4 = select(T.sel4[:, :], T.onesb[:, 0:4], [[32, 4]], A.is_equal, 0.0, 0)
-    c_h0 = select(T.Qhi[:, 0:256:2], T.onesb[:, :], [[1, 2], [2, 8], [32, 8]], A.is_equal, 0.0, -128)
-    wait("g", k1)
-    send_two("h0_%d", lambda k: T.KS[:, 64 * order[k]:64 * order[k] + 64], T.KR[:, 64 * q:64 * q + 64], "gone")
-    wait("y", "gone")
-    bulk(BULK[0], BULK[1])
-
-    wait("g", m_one)
-    wait("g", c_4, c_h0)
-    c_h = select(T.Qhi[:, 0:256:2], T.Qhi[:, 0:256:2], [[1, 2], [2, 8], [32, 8]], A.not_equal, 1.0, 16 - 128)
-    c_4 = select(T.sel4[:, :], T.sel4[:, :], [[32, 4]], A.not_equal, 1.0, 16)
-    c_idb = select(T.idb[:, :], T.onesb[:, :], [[1, 128]], A.is_equal, 0.0, 0)
-    c_q = new()
-    for h in range(2):
-        select(T.Qlo[:, 128 * h:128 * h + 128], T.onesb[:, :], [[2, 8], [16, 16]], A.is_equal, 0.0, h, s=c_q)
-    pat = [[1, 8], [8, 16]]
-    c_m = select(T.mats[:, 256:384], T.onesb[:, :], pat, A.is_equal, 0.0, 0)
-    wait("g", z_w1)
-    select(T.mats[:, 0:128], zb, pat, A.is_gt, -1.0, 0, s=c_m)
-    select(T.mats[:, 128:256], zb, pat, A.is_ge, -1.0, 0, s=c_m)
-
-    wait("s", z_w1, m_one)
-    m_mel = new()
-    for k in range(2):
-        ev(S.activation(T.MEL[:, 16 * k:16 * k + 16, 0:8], zb, AF.Copy), 1, m_mel)
-    ev(S.activation(T.Qhi[:, 1:256:2], zb, AF.Copy), 1, m_mel)
-    s_mel = ev(S.activation(T.MEL[:, :, 15], T.onesb[:, 0:32], AF.Copy))
-    ev(S.activation(T.MEL[:, :, 8:16:2], T.onesb[:, :], AF.Copy, scale=-BIG * 17 / 16), 1, s_mel)
-    wait("v", v_k)
-    v_kf = ev(V.tensor_scalar(out=T.kf[:, 0:1], in0=T.kb[:, 0:1], scalar1=15.0 / 256, scalar2=1.0 / 16, op0=A.mult,
-                              op1=A.add))
-    ev(V.tensor_copy(T.kf[:, 1:2], T.kb[:, 1:2]), 1, v_kf)
-    kef = T.kf[:, 0:1]
-    wait("v", v_kf)
+    ev(V.tensor_scalar(out=T.kf[:, 0:1], in0=T.kb[:, 0:1], scalar1=15.0 / 256, scalar2=1.0 / 16, op0=A.mult,
+                       op1=A.add), 1, v_kf)
+    ev(V.tensor_copy(T.kf[:, 1:3], T.kb[:, 1:3]), 1, v_kf)
+    kef, pm, pp = (T.kf[:, x:x + 1] for x in (0, 2, 3))
+    k_own = keys(q, T.KR, q, new())
+    wait("v", v_kf, v_lo)
     v_hi = ev(V.tensor_scalar(out=T.fhib[:, :], in0=T.fkt[:, :], scalar1=BIG - 255.5, scalar2=kef, op0=A.add,
                               op1=A.mult))
-    v_lo = ev(V.tensor_scalar(out=T.flo[:, :], in0=T.fkt[:, :], scalar1=511, scalar2=None, op0=A.bitwise_and))
-    k_own = keys(q, T.KR, new())
-    wait("v", v_lo, c_j)
     v_lo = ev(V.tensor_scalar(out=T.flob[:, :], in0=T.flo[:, :], scalar1=-256.0, scalar2=kef, op0=A.add, op1=A.mult))
+    d_pw = new()
+    for a in range(4):
+        wait(PWQ[a % 2], v_ps, z1, z2)
+        ev(queues[PWQ[a % 2]].dma_start(T.pw[32 * a:32 * a + 32:16, :], T.ps[0:64, :]), 16, d_pw)
+    wait("g", k0)
+    send(0, "h0_0", T.KS[:, 0:64], T.KR[:, 64 * q:64 * q + 64])
+    if LATE:
+        first(0, 0, CX)
+    consts(GORD[1])
+    wait("g", k1)
+    send_two("h0_%d", lambda k: T.KS[:, 64 * k:64 * k + 64], T.KR[:, 64 * q:64 * q + 64], "gone")
+    consts(GORD[4])
+    first(1, 0, R)
+    if CX < R:
+        first(0, CX, R)
+    if BE:
+        wait("y", d_pw)
+        bulk((1, XP, XP + BE))
+    wait("y", "gone")
+    bulk((2, x0, x0 + BQ), (3, x0, x0 + B3), (1, XP + BE, B1))
+    consts(GORD[2])
+
+    wait("s", m_one)
+    s_mel = new()
+    for k in range(2):
+        ev(S.activation(T.MEL[:, 16 * k:16 * k + 16, 0:8], T.onesb[:, :], AF.Copy, scale=0.0), 1, s_mel)
+    ev(S.activation(T.MEL[:, :, 15], T.onesb[:, 0:32], AF.Copy), 1, s_mel)
+    ev(S.activation(T.MEL[:, :, 8:16:2], T.onesb[:, :], AF.Copy, scale=-BIG * 17 / 16), 1, s_mel)
     wait("s", v_mb)
     for h in range(2):
         for x in range(3):
             ev(S.activation(T.MEL[:, 16 * h:16 * h + 16, 9 + 2 * x], T.meb[:, 32 * x + h:32 * x + 32:2], AF.Copy,
                             scale=16384.0 if x == 0 else 1.0), 1, s_mel)
 
-    KB = (T.b0, T.b7)
-
-    def high(h):
-        wait("p", v_hi, c_h, m_mel)
-        PE.matmul(KB[h][:, 0:256], T.Qhi[:, 128 * h:128 * h + 128], T.fhib[:, :], True, False)
-
-    def measure(h):
-        wait("p", s_mel, c_idb)
+    def rows(h):
+        wait("p", v_hi, v_lo, c_q, s_mel, cs["i"])
+        out = T.b0[:, 256 * h:256 * h + 256]
+        PE.matmul(out, T.Qhi[:, 128 * h:128 * h + 128], T.fhib[:, :], True, False)
         for x in range(2):
-            PE.matmul(KB[h][:, x:256:2], T.MEL[:, 16 * h + 8 * x:16 * h + 8 * x + 8, :], T.idb[:, :], False, False)
-
-    def low(h):
-        wait("p", v_lo, c_q)
-        return ev(PE.matmul(KB[h][:, 0:256], T.Qlo[:, 128 * h:128 * h + 128], T.flob[:, :], False, True))
+            PE.matmul(T.b0[:, 256 * h + x:256 * h + 256:2], T.MEL[:, 16 * h + 8 * x:16 * h + 8 * x + 8, :], T.idb[:, :],
+                      False, False)
+        return PE.matmul(out, T.Qlo[:, 128 * h:128 * h + 128], T.flob[:, :], False, True)
 
     turn = order + [q]
-    CB = [T.b1, T.b2, T.b4, T.b5]
+    CB = [T.b1, T.b2, T.b1, T.b5]
+    out_of = []
     wait("v", d_pw, z3)
     wait("s", d_pw, z3)
-    wait("p", c_4, v_ps)
-    high(0)
+    wait("p", v_ps)
     done = [new() for n in range(4)]
+    c_q = new()
 
     def evacuate(k):
         wait("v", done[k])
-        wait("g", ev(V.tensor_copy(T.CS[:, 32 * k:32 * k + 32], CB[k][:, 0:32])))
+        out = T.CS[:, 32 * k:32 * k + 32]
+        out_of.append(ev(V.tensor_scalar(out=out, in0=CB[k][:, 0:32], scalar1=-1.0, scalar2=7.5, op0=A.mult, op1=A.add)
+                         if k == 2 else V.tensor_copy(out, CB[k][:, 0:32])))
+        wait("g", out_of[k])
         send(k, "h1_%d" % k, T.CS[:, 32 * k:32 * k + 32], T.CR[:, 32 * k:32 * k + 32])
 
     for n in range(4):
         r = turn[n]
         got = []
+        if n == 3:
+            for h in range(2):
+                for Q, base, col in ((T.Qhi, h - 128.0, pm), (T.Qlo, float(h), pp)):
+                    ev(V.tensor_scalar(out=Q[:, 128 * h:128 * h + 128], in0=T.X1[:, :], scalar1=base, scalar2=col,
+                                       op0=A.add, op1=A.is_equal), 1, c_q)
+            evacuate(2)
+            rows(0)
+            p_k = ev(rows(1))
         for k, runs in zip("vs", ROUNDS[n]):
             wait(k, "h0_%d" % n if n < 3 else k_own)
             for x, (lo, hi) in enumerate(runs):
                 out = T.Pg[:, 1024 * n + 16 * lo:1024 * n + 16 * hi]
                 win = T.pw[:, :].indirect(T.KR[:, 64 * r + lo:64 * r + hi])
                 got.append((lo, hi, ev(V.tensor_copy(out, win) if k == "v" else S.activation(out, win, AF.Copy))))
-                if k == "v" and n and x == (0 if n == 3 else len(runs) - 1):
+                if k == "v" and n in (1, 2) and x == len(runs) - 1:
                     evacuate(n - 1)
+                if k == "v" and n == 0:
+                    wait("v", cs["1"])
+                    wait("p", ev(V.tensor_scalar(out=T.sel4[:, :], in0=T.X1[:, 0:8:2], scalar1=pm, scalar2=None,
+                                                 op0=A.is_equal)))
+        if n == 2:
+            wait("p", out_of[0])
         for u in BLOCKS:
             wait("p", *[e for lo, hi, e in got if lo < 16 * u + 16 and hi > 16 * u])
             for h in range(2):
-                ev(PE.matmul(CB[n][:, 16 * h + u:16 * h + 16:4],
-                             T.Pg[:, 1024 * n + 256 * u + h:1024 * n + 256 * u + 256:2], T.sel4[:, :], True, True),
-                   1, done[n])
-        if n == 0:
-            high(1)
-        if n == 1:
-            measure(0)
-        if n == 2:
-            measure(1)
-            p_k = [low(h) for h in range(2)]
+                i = PE.matmul(CB[n][:, 16 * h + u:16 * h + 16:4],
+                              T.Pg[:, 1024 * n + 256 * u + h:1024 * n + 256 * u + 256:2], T.sel4[:, :],
+                              n < 3 or (u == BLOCKS[0] and h == 0), n < 3)
+                if n < 3:
+                    ev(i, 1, done[n])
+        if n == 3:
+            for k in range(2):
+                wait("p", "h1_%d" % k)
+                i = PE.matmul(CB[3][:, 0:32], T.idb[:, :], T.CR[:, 32 * k:32 * k + 32], False, k == 1)
+            ev(i, 1, done[3])
     g.sem_inc(T.sem.issued, 1)
     total["issued"] = 1
-    wait("y", "issued", *[e for lo, hi, e in got])
-    z_w2 = ev(SY.dma_start(T.pw[0:128:16, 0:C], T.pw[1:128:16, 0:C]), 16)
-    bulk(BULK[1], 8)
-    s_k1 = new()
-    for h in range(2):
-        wait("s", p_k[h])
-        ev(S.activation(T.K1[:, 256 * h:256 * h + 256], KB[h][:, 0:256], AF.Copy), 1, s_k1)
-    wait("v", "h1_0", "h1_1")
-    t = ev(V.tensor_tensor(T.thr[:, 0:32], T.CR[:, 0:32], T.CR[:, 32:64], A.add))
-    v_j = ev(V.tensor_scalar(out=T.J[:, 0:32], in0=T.rowj[:, :], scalar1=T.kf[:, 1:2], scalar2=0.25, op0=A.add,
-                             op1=A.mult))
-    ev(V.tensor_scalar(out=T.J[:, 32:64], in0=T.rowj[:, :], scalar1=T.kf[:, 1:2], scalar2=-0.25, op0=A.add,
-                       op1=A.mult), 1, v_j)
-    wait("v", t)
-    t = ev(V.tensor_scalar(out=T.thr[:, 32:64], in0=T.thr[:, 0:32], scalar1=-1.0, scalar2=7.5, op0=A.mult, op1=A.add))
-    m_w = ev(V.memset(T.ATW[:, 0:PAD], 0))
-    wait("v", t, done[3])
-    t = ev(V.tensor_tensor(T.thr[:, 64:96], T.thr[:, 32:64], CB[3][:, 0:32], A.subtract))
+    consts(GORD[3])
+    wait("y", done[0], done[1])
+    z_w2 = ev(SY.dma_start(T.Pg[0:128:16, 0:C], T.pw[1:128:16, 0:C]), 16)
+    if XP:
+        wait("y", d_c[1])
+        d_cb = ev(SY.dma_start(T.ATW[16:32, PAD:PAD + XP], T.ATW[64:80, PAD:PAD + XP]), 16)
+    bulk((5, XP, x0))
+    wait("y", "issued")
+    bulk((5, x0, R), (1, B1, R), (2, x0 + BQ, R), (3, x0 + B3, R), (6, x0, R), (7, x0, R))
+    wait("s", p_k)
+    s_k1 = ev(S.activation(T.K1[:, :], T.b0[:, :], AF.Copy))
+    wait("v", cs["2"], cs["j"])
+    c_m = ev(V.tensor_scalar(out=T.mats[:, 256:384], in0=T.X2[:, :], scalar1=pp, scalar2=None, op0=A.is_equal))
+    for x, op in enumerate((A.is_le, A.is_lt)):
+        ev(V.tensor_scalar(out=T.mats[:, 128 * x:128 * x + 128], in0=T.X2[:, :], scalar1=pp, scalar2=-1.0, op0=op,
+                           op1=A.mult), 1, c_m)
+    v_j = new()
+    for x, w in enumerate((0.25, -0.25)):
+        ev(V.tensor_scalar(out=T.J[:, 32 * x:32 * x + 32], in0=T.rowj[:, :], scalar1=T.kf[:, 1:2], scalar2=w, op0=A.add,
+                           op1=A.mult), 1, v_j)
     L1, L1B, IP, ONE = T.mats[:, 0:128], T.mats[:, 128:256], T.mats[:, 256:384], T.onesb[:, :]
     wait("p", c_m, v_j)
     PE.matmul(T.b3[:, 0:32], IP, T.J[:, 0:32], True, False)
 
-    c_r = select(T.R16[0:16, :], T.onesb[0:16, 0:16], [[8, 2], [1, 2], [2, 4]], A.is_equal, 0.0, 0)
-    c_rep = select(T.rep[0:16, :], T.onesb[0:16, :], [[0, 8], [1, 16]], A.is_equal, 0.0, 0)
-    wait("g", c_r)
-    c_r = select(T.R16[0:16, 0:4], T.R16[0:16, 0:4], [[2, 4]], A.not_equal, 1.0, 8)
-    for lo, w in ((4, 256.0 + PAD), (8, -240.0)):
-        select(T.R16[0:16, lo:lo + 4], T.R16[0:16, lo:lo + 4], [[0, 4]], A.not_equal, w, 15, s=c_rep)
-    c_s1 = select(T.sele[:, :], T.onesb[:, 0:64], [[16, 2], [1, 16], [32, 2]], A.is_equal, 0.0, 0)
-    wait("g", c_r)
-    select(T.R16[0:16, 0:4], T.R16[0:16, 0:4], [[0, 4]], A.not_equal, (256.0 + PAD) / 16, 15, s=c_rep)
-    wait("g", c_s1)
-    c_sel = select(T.sele[:, :], T.sele[:, :], [[16, 2], [1, 16], [32, 2]], A.not_equal, 1.0, 64)
-
-    wait("v", t, "h1_2")
-    v_m = ev(V.tensor_tensor(T.Msk[:, :], T.CR[:, 64:96], T.thr[:, 64:96], A.is_gt))
+    wait("v", done[3], "h1_2")
+    v_m = ev(V.tensor_tensor(T.Msk[:, :], CB[3][:, 0:32], T.CR[:, 64:96], A.is_gt))
     wait("v", v_m, v_j)
     v_sc = ev(V.tensor_tensor_scan(T.Sc[:, :], T.Msk[:, 0:16], T.Msk[:, 16:32], 0.0, A.add, A.add))
     v_mj = ev(V.tensor_tensor(T.MJ[:, :], T.Msk[:, :], T.J[:, 32:64], A.mult))
+    m_w = ev(V.memset(T.ATW[:, 0:PAD], 0.0))
     wait("p", v_m)
     PE.matmul(T.b3[:, 0:32], L1, T.Msk[:, :], False, False)
     PE.matmul(T.b3[:, 0:16], L1, T.Msk[:, 16:32], False, False)
@@ -332,40 +407,50 @@ def rank_program(g, core, T, topo):
     PE.matmul(T.b3[:, 16:32], ONE, T.Sc[:, :], False, False)
     wait("p", v_mj)
     p_pos = ev(PE.matmul(T.b3[:, 0:32], IP, T.MJ[:, :], False, True))
-    wait("p", s_k1)
-    p_nt = ev(PE.matmul(T.b7[:, 256:257], ONE, T.Sc[:, 15:16], True, True))
-    wait("p", c_rep)
+    p_nt = ev(PE.matmul(T.b5[:, 256:257], ONE, T.Sc[:, 15:16], True, True))
+    if NP[0]:
+        p_sp = spread(T.b4, 0, NP[0])
+    wait("p", cs["r"], out_of[2])
     p_rl = ev(PE.matmul(T.b1[:, 0:16], T.rep[0:16, :], T.R16[0:16, :], True, True))
     wait("v", p_pos)
     v_o3 = ev(V.tensor_copy(T.off3[:, :], T.b3[:, 0:32]))
     wait("s", p_nt)
-    s_nt = ev(S.activation(T.nt[:, :], T.b7[:, 256:257], AF.Copy))
+    s_nt = ev(S.activation(T.nt[:, :], T.b5[:, 256:257], AF.Copy))
+    repeat("s", 0, RS1)
     wait("s", p_rl)
     s_rl = ev(S.activation(T.RL[:, :], T.b1[:, 0:16], AF.Copy))
     s_r1 = ev(S.activation(T.rm3[:, 0:3], T.b1[:, 12:15], AF.Copy, accum_out=T.rm1[:, :]))
+    if NP[0]:
+        put("s", p_sp, T.b4, 0, NP[0])
     wait("s", s_r1)
     s_rm = ev(S.activation(T.RM[:, :], T.onesb[:, 0:16], AF.Copy, scale=T.rm1[:, :]))
+    repeat("s", RS1, RS)
+    if RG:
+        wait("g", cs["s"], cs["r"])
+        repeat("g", RS, RS + RG)
 
     wait("v", v_o3, s_k1, z_w2)
-    v_w1 = ev(V.tensor_copy(T.pw[:, 0:3584].indirect(T.off3[:, :]), T.K1[:, :]))
-    wait("p", v_w1, s_rl)
+    v_w1 = ev(V.tensor_copy(T.Pg[:, 0:3584].indirect(T.off3[:, :]), T.K1[:, :]))
+    wait("p", v_w1, s_rl, out_of[1])
     p_l = new()
     for c in range(6):
         for j1 in range(2):
             y = 4 * (c // 2) + 2 * j1 + c % 2
-            ev(PE.matmul(T.b4[:, y:144:12], T.pw[:, 768 * j1 + c:768 * j1 + 768:6], T.RL[:, 0:12], True, True), 1, p_l)
+            ev(PE.matmul(T.b2[:, y:144:12], T.Pg[:, 768 * j1 + c:768 * j1 + 768:6], T.RL[:, 0:12], True, True), 1, p_l)
+    if NP[1]:
+        p_sp = spread(T.b7, 128 * NP[0], NP[1])
     wait("s", v_w1)
     wait("v", v_w1)
     s_w2 = [new() for ch in range(3)]
     for c in range(6):
         for jb in range(4):
-            out, in_ = T.W2[:, c // 2, :, jb, c % 2, :], T.pw[:, 384 * jb + c:384 * jb + 384:6]
+            out, in_ = T.W2[:, c // 2, :, jb, c % 2, :], T.Pg[:, 384 * jb + c:384 * jb + 384:6]
             ev(V.tensor_copy(out, in_) if 4 * c + jb < WV else S.activation(out, in_, AF.Copy), 1, s_w2[c // 2])
     wait("v", p_l)
-    v_z = ev(V.tensor_scalar(out=T.Z[:, :], in0=T.b4[:, 96:144], scalar1=ROUND, scalar2=ROUND, op0=A.add,
+    v_z = ev(V.tensor_scalar(out=T.Z[:, :], in0=T.b2[:, 96:144], scalar1=ROUND, scalar2=ROUND, op0=A.add,
                              op1=A.subtract))
     wait("v", v_z)
-    v_t = [ev(V.tensor_tensor(T.T2[:, 48 * e:48 * e + 48], T.b4[:, 48 * e:48 * e + 48], T.Z[:, :],
+    v_t = [ev(V.tensor_tensor(T.T2[:, 48 * e:48 * e + 48], T.b2[:, 48 * e:48 * e + 48], T.Z[:, :],
                               A.add if e else A.subtract)) for e in range(2)]
     v_lu = new()
     for e in range(2):
@@ -374,66 +459,92 @@ def rank_program(g, core, T, topo):
             ev(V.tensor_scalar(out=T.Ls[64 * e:64 * e + 64, :, j0, :], in0=T.T2[64 * j0:64 * j0 + 64, 48 * e:48 * e + 48],
                                scalar1=1.0 if e else 16.0, scalar2=None, op0=A.mult), 1, v_lu)
     wait("g", v_lu)
-    send(0, "h2_0", T.Ls[:, 6 * order[0]:6 * order[0] + 6, :, :], T.Lr[:, 24 * q:24 * q + 24])
-    send_two("h2_%d", lambda k: T.Ls[:, 6 * order[k]:6 * order[k] + 6, :, :], T.Lr[:, 24 * q:24 * q + 24])
-    wait("g", s_nt)
-    ev(g.dma_start(T.y[:, C:C + 1], T.nt[0:16, :], allow_slow_non_contiguous=True), 16)
+    for k in range(3):
+        send(k, "h2_%d" % k, T.Ls[:, 6 * order[k]:6 * order[k] + 6, :, :], T.Lr[:, 24 * q:24 * q + 24])
 
-    wait("p", s_rm)
+    wait("p", s_rm, s_nt)
     for ch in range(3):
         wait("p", s_w2[ch])
         for a in range(4):
             c0 = 64 * ch + 32 * (a % 2) + a // 2
             PE.matmul(T.b5[:, c0:c0 + 31:2], T.W2[:, ch, a, :, :, :], T.RM[:, :], ch + a == 0, False)
+    if RV:
+        repeat("v", RS + RG, RS + RG + RV)
+    if NP[1]:
+        put("v", p_sp, T.b7, 128 * NP[0], NP[1])
     wait("v", v_lu)
     v_own = ev(V.tensor_copy(T.Lr[:, 24 * q:24 * q + 24], T.Ls[:, 6 * q:6 * q + 6, :, :]))
-    wait("v", v_own, d_at, m_w)
-    wait("p", c_sel, s_nt, s_k1, s_rl, s_r1)
+    wait("v", d_at, d_a1, r_at, m_w, *d_c)
+    wait("s", d_at, d_a1, r_at, m_w, *d_c)
+    wait("p", cs["s"], s_k1, s_rl, s_r1, v_o3)
 
-    def gather(r, lo, hi, out, done=None):
-        e = ev(V.tensor_copy(T.G[:, 384 * r + 128 * lo:384 * r + 128 * hi],
-                             T.ATW[:, :].indirect(T.Lr[:, 24 * r + 8 * lo:24 * r + 8 * hi])))
-        wait("p", e)
-        done = done or new()
-        for ch in range(lo, hi):
-            i = PE.matmul(out[:, 64 * ch:64 * ch + 64], T.G[:, 384 * r + 128 * ch:384 * r + 128 * ch + 128],
-                          T.sele[:, :], r != q, r != q or ch == 2)
-            if r != q or ch == 2:
+    def gather(k, r, lo, hi):
+        out = T.G[:, 384 * r + 16 * lo:384 * r + 16 * hi]
+        win = T.ATW[:, :].indirect(T.Lr[:, 24 * r + lo:24 * r + hi])
+        return lo, hi, ev(V.tensor_copy(out, win) if k == "v" else S.activation(out, win, AF.Copy))
+
+    def add_up(tile, got, chunks, bank, start=True, stop=True):
+        done = new()
+        for ch in chunks:
+            wait("p", *[e for lo, hi, e in got if lo < 8 * ch + 8 and hi > 8 * ch])
+            i = PE.matmul(bank[:, 64 * ch:64 * ch + 64], tile[:, 128 * ch:128 * ch + 128], T.sele[:, :], start,
+                          stop and (start or ch == 2))
+            if stop and (start or ch == 2):
                 ev(i, 1, done)
         return done
 
-    gather(q, 0, 1, T.b5)
-    p_own = gather(q, 1, 3, T.b5)
-    wait("v", "h2_0")
-    s = []
-    for lo, hi, b in ((0, 1, T.b3), (1, 2, T.b7), (2, 3, T.b2)):
-        wait("s", gather(order[0], lo, hi, b))
-        s.append(ev(S.activation(T.S0[:, 64 * lo:64 * hi], b[:, 64 * lo:64 * hi], AF.Copy)))
-    wait("g", *s)
-    send(0, "h3_0", T.S0[:, :], T.L0[:, :])
-    wait("v", "h2_1")
-    p1 = gather(order[1], 1, 3, T.b1, gather(order[1], 0, 1, T.b1))
-    wait("v", "h2_2")
-    pa = gather(order[2], 0, 2, T.b0)
-    pb = gather(order[2], 2, 3, T.b4)
-    for p, rsem, k, out, bank, dst, lo, hi in ((p1, "h3_1", 1, T.S1, T.b1, T.L1[:, :], 0, 192),
-                                               (pa, "h3_2", 2, T.S2, T.b0, T.L2[:, 0:4, :, :], 0, 128),
-                                               (pb, "h3_3", 2, T.S2, T.b4, T.L2[:, 4:6, :, :], 128, 192)):
+    def tile(r):
+        return T.G[:, 384 * r:384 * r + 384]
+
+    wait("s", v_own)
+    wait("v", v_own)
+    if OWNF:
+        add_up(tile(q), [gather("v", q, 0, OWNF)] + ([gather("s", q, OWNF, 24)] if OWNF < 24 else []), (2, 0, 1), T.b5,
+               False, False)
+    got = []
+    for k in range(3):
+        got.append([])
+        for x, runs in zip("vs", SPLIT[k]):
+            wait(x, "h2_%d" % k)
+            got[k] += [gather(x, order[k], lo, hi) for lo, hi in runs]
+    wait("g", *[e for lo, hi, e in got[0]])
+    send(0, "h3_0", tile(order[0]), T.L0[:, :])
+    if RAW1:
+        wait("g", *[e for lo, hi, e in got[1]])
+        send(1, "h3_1", tile(order[1]), T.L1[:, :])
+        parts = []
+    else:
+        parts = [(1, add_up(tile(order[1]), got[1], CH[0], T.b1), "h3_1", T.b1, T.S1, T.L1[:, 0:192], 0, 192)]
+    if TWO:
+        parts += [(2, add_up(tile(order[2]), got[2], (0, 1), T.b0), "h3_2", T.b0, T.S2, T.L2[:, 0:4, :, :], 0, 128),
+                  (2, add_up(tile(order[2]), got[2], (2,), T.b2), "h3_3", T.b2, T.S2, T.L2[:, 4:6, :, :], 128, 192)]
+    else:
+        parts += [(2, add_up(tile(order[2]), got[2], CH[1], T.b0), "h3_2", T.b0, T.S2, T.L2[:, :, :, :], 0, 192)]
+    if not OWNF:
+        own = [gather("s", q, 8 * x, 8 * x + 8) for x in range(3)]
+    for k, p, rsem, bank, out, dst, lo, hi in parts:
         wait("v", p)
         wait("g", ev(V.transpose(out[:, lo:hi], bank[:, lo:hi])))
         send(k, rsem, out[:, lo:hi], dst)
+    if not OWNF:
+        add_up(tile(q), own, range(3), T.b5, False, False)
+    wait("p", "h3_0")
+    a = add_up(T.L0, [], range(3), T.b5, False, not RAW1)
+    if RAW1:
+        wait("p", "h3_1")
+        a = add_up(T.L1, [], range(3), T.b5, False, True)
+    wait("g", s_nt)
+    ev(g.dma_start(T.y[:, C:C + 1], T.nt[0:16, :], allow_slow_non_contiguous=True), 16)
 
-    acc = T.b5[:, 0:192]
-    wait("v", p_own, "h3_0")
-    a = ev(V.tensor_tensor(acc, acc, T.L0[:, :], A.add))
     wait("v", a)
-    a = ev(V.transpose(T.bT[:, 0:6, :, :], acc))
-    wait("v", a, "h3_1")
-    a = ev(V.tensor_tensor(T.bT[:, 0:6, :, :], T.bT[:, 0:6, :, :], T.L1[:, :], A.add))
+    a = ev(V.transpose(T.bT[:, 0:6, :, :], T.b5[:, 0:192]))
+    if not RAW1:
+        wait("v", a, "h3_1")
+        a = ev(V.tensor_tensor(T.bT[:, 0:6, :, :], T.bT[:, 0:6, :, :], T.L1[:, 0:192], A.add))
     x = new()
     for c in range(6):
         ch, xl = c // 2, c % 2
-        wait("v", a, "h3_3" if ch == 2 else "h3_2")
+        wait("v", a, "h3_3" if ch == 2 and TWO else "h3_2")
         ev(V.tensor_tensor(T.O[:, c:192:6], T.bT[:, 2 * ch:2 * ch + 2, xl, :], T.L2[:, 2 * ch:2 * ch + 2, xl, :], A.add),
            1, x)
     for n, jbs in (("y", (0, 1)), ("s", (2, 3))):

from concourse.bass import DstId, RemoteDMATransfer
from concourse.mybir import AluOpType as A, ActivationFunctionType as AF

R, F, C, D, NR = 8192, 4096, 1536, 2, 4
PU, PV, PS, PG = 2304, 3200, 5888, 5888
RS, RG, RV = 704, 0, 128
RS1 = 320
NP = (3, 1)
BE, BQ = 4096, 4608
CX, B1, B3 = R, R, 0
GORD = ("", "", "i2j", "mrs", "1")
LATE = False
SPLIT = ((((0, 12),), ((12, 24),)), (((0, 8), (16, 20)), ((8, 16), (20, 24))), (((0, 8),), ((8, 16), (16, 24))))
CH = ((0, 1, 2), (0, 1, 2))
TWO = True
OWNF = 12
RAW1 = False
PWQ = "yy"
PAD = 8
BIG = 1.5 * 2.0 ** 16
ROUND = 1.5 * 2.0 ** 32
ROUNDS = ((((0, 30),), ((30, 64),)), (((0, 30),), ((30, 64),)), (((0, 16), (16, 32)), ((48, 64), (32, 48))),
          (((0, 24),), ((48, 64), (24, 48))))
BLOCKS = (3, 0, 2, 1)
WV = 6

SCRATCH = {
    "limi": ("sbuf", [128, 4], "int32"), "limf": ("sbuf", [128, 4], "float32"), "onesf": ("sbuf", [128, 32], "float32"),
    "X1": ("sbuf", [128, 128], "bfloat16"), "X2": ("sbuf", [128, 128], "bfloat16"),
    "a0": ("sbuf", [128, 256], "int32"), "ps": ("sbuf", [128, 256], "bfloat16"),
    "pw": ("sbuf", [128, R], "bfloat16"), "Pg": ("sbuf", [128, F], "bfloat16"),
    "kc": ("sbuf", [128, 1], "int32"), "kb": ("sbuf", [128, 4], "int32"), "kf": ("sbuf", [128, 4], "bfloat16"),
    "fkt": ("sbuf", [128, 256], "int32"),
    "KS": ("sbuf", [128, 192], "uint16"), "KR": ("sbuf", [128, 256], "uint16"),
    "sel4": ("sbuf", [128, 4], "bfloat16"),
    "CS": ("sbuf", [128, 96], "bfloat16"), "CR": ("sbuf", [128, 96], "bfloat16"),
    "flo": ("sbuf", [128, 256], "int32"),
    "fhib": ("sbuf", [128, 256], "bfloat16"), "flob": ("sbuf", [128, 256], "bfloat16"),
    "K1": ("sbuf", [128, 512], "bfloat16"),
    "W2": ("sbuf", [128, 3, 4, 4, 2, 16], "bfloat16"),
    "mei": ("sbuf", [128, 32], "int32"), "mep": ("sbuf", [128, 96], "int32"), "meb": ("sbuf", [128, 96], "bfloat16"),
    "MEL": ("sbuf", [128, 32, 16], "bfloat16"),
    "onesb": ("sbuf", [128, 128], "bfloat16"), "idb": ("sbuf", [128, 128], "bfloat16"),
    "Qlo": ("sbuf", [128, 256], "bfloat16"), "Qhi": ("sbuf", [128, 256], "bfloat16"),
    "rowj": ("sbuf", [128, 32], "float32"), "J": ("sbuf", [128, 64], "float16"),
    "mats": ("sbuf", [128, 384], "bfloat16"), "sele": ("sbuf", [128, 64], "float32"),
    "rep": ("sbuf", [128, 128], "bfloat16"), "R16": ("sbuf", [128, 16], "bfloat16"),
    "RL": ("sbuf", [128, 16], "bfloat16"), "RM": ("sbuf", [128, 16], "bfloat16"),
    "rm3": ("sbuf", [128, 4], "float32"), "rm1": ("sbuf", [128, 1], "float32"),
    "Msk": ("sbuf", [128, 32], "float16"), "Sc": ("sbuf", [128, 16], "float16"),
    "MJ": ("sbuf", [128, 32], "float16"), "off3": ("sbuf", [128, 32], "uint16"),
    "Rm": ("sbuf", [128, 128], "float32"),
    "nt": ("sbuf", [128, 1], "float32"),
    "Z": ("sbuf", [128, 48], "float32"), "T2": ("sbuf", [128, 96], "float32"),
    "Ls": ("sbuf", [128, 24, 2, 2], "uint16"), "Lr": ("sbuf", [128, NR * 24], "uint16"),
    "ATW": ("sbuf", [128, R + PAD], "float32"), "G": ("sbuf", [128, C], "float32"),
    "S1": ("sbuf", [128, 192], "float32"), "S2": ("sbuf", [128, 192], "float32"),
    "L0": ("sbuf", [128, 384], "float32"), "L1": ("sbuf", [128, 384], "float32"),
    "L2": ("sbuf", [128, 6, 2, 16], "float32"), "O": ("sbuf", [128, 192], "float32"),
    "bT": ("psum", [128, 16, 2, 16], "float32"),
}
for _b in (0, 1, 2, 3, 4, 5, 7):
    SCRATCH["b%d" % _b] = ("psum", [128, 512], "float32")
NEV = 132
SEMAPHORES = (["e%d" % _i for _i in range(NEV)] + ["left", "issued", "gone", "h3_3"]
              + ["h%d_%d" % (_h, _k) for _h in range(4) for _k in range(3)])


def rank_program(g, core, T, topo):
    q = T.rank_of(core)
    if q is None:
        return
    V, S, PE, SY = g.vector, g.scalar, g.tensor, g.sync
    queues = {"g": g, "v": V, "s": S, "p": PE, "y": SY}
    used, total, seen, waited = [0], {}, {}, {}

    def new():
        s = "e%d" % used[0]
        used[0] += 1
        total[s] = 0
        return s

    def ev(inst, n=1, s=None):
        if s is None:
            s = new()
        inst.then_inc(T.sem[s], n)
        total[s] += n
        return s

    def wait(k, *names):
        for s in names:
            n = total[s]
            if seen.get((k, s), 0) < n:
                queues[k].wait_ge(T.sem[s], n)
                seen[(k, s)] = n
                waited[s] = max(waited.get(s, 0), n)

    mine = [c for c in T.cores if topo.die(c) == topo.die(core)]
    far = [c for c in T.cores if topo.die(c) != topo.die(core)]
    at = mine.index(core)
    partners = [far[at], far[1 - at], mine[1 - at]]
    order = [T.rank_of(c) for c in partners]
    for k in range(3):
        total["h0_%d" % k] = 8 if k else 16
        total["h1_%d" % k] = total["h2_%d" % k] = total["h3_%d" % k] = 16
    if TWO:
        total["h3_3"] = 16

    def transfer(c, engines, rsem, src, dst, left="left"):
        rid, pid, _ = topo.addr(c)
        total[left] = total.get(left, 0) + len(engines)
        return RemoteDMATransfer(dst_ids=[DstId(rid=rid, pnc=pid)], dma_engine_mask=sum(1 << e for e in engines),
                                 remote_sem=T.sem[rsem], src=src, dst=dst)

    def send(k, rsem, src, dst, left="left"):
        rid, pid, _ = topo.addr(partners[k])
        total[left] = total.get(left, 0) + len(topo.engines(core, partners[k]))
        g.remote_dma(dst, src, T.sem[rsem], T.sem[left], pid, rid, topo.mask(core, partners[k]))

    def send_two(rsem, src, dst, left="left"):
        g.remote_dma_fused([transfer(partners[k], topo.engines(core, partners[k])[k - 1::2], rsem % k, src(k), dst, left)
                            for k in (1, 2)], local_sem=T.sem[left])

    def iota(out, pattern, base=0, cm=0):
        return g.iota(out, pattern, base, cm, allow_small_or_imprecise_dtypes=True)

    def select(out, in_, pattern, op, fill, base, cm=-1, s=None):
        return ev(g.affine_select(out, in_, pattern, op, fill, base, cm), 1, s)

    d_fk = ev(S.dma_start(T.fkt[:, :], T.fk[:, :]), 16)
    d_lim = ev(SY.dma_start(T.limi[0:1, :], T.lim[0:1, :]), 16)
    d_a0 = ev(SY.dma_start(T.a0[0:64, :], T.at[0:1, :]), 16)
    d_me = ev(SY.dma_start(T.mei[:, :], T.me[0:1, :]), 16)

    n = (R - PG) // 2
    zs = ev(V.memset(T.pw[:, 0:256], 0.0))
    z0 = ev(V.memset(T.pw[:, 256:n], 0.0))
    m_one = ev(V.memset(T.onesb[:, :], 1.0))
    m_of = ev(V.memset(T.onesf[0:1, :], 1.0))
    z1 = ev(V.memset(T.pw[:, n:PU], 0.0))
    c_io = ev(g.iota(T.kc[:, :], [[0, 1]], 0, 1))
    wait("y", zs, z0)
    wait("s", zs)
    z2, z3 = new(), new()
    for k in range(2):
        ev(SY.dma_start(T.pw[1:128:2, PG + n * k:PG + n * k + n], T.pw[1:128:2, 0:n]), 16, z3)
    for step in (4, 8, 16):
        ev(SY.dma_start(T.pw[step // 2:128:step, PG:R], T.pw[1:512 // step:2, 0:n]), 16, z3)

    XP = 128 * sum(NP)
    x0 = XP + RS + RG + RV
    d_at, d_a1, r_at = new(), new(), new()
    d_c = []

    def first(e, lo, hi):
        d_c.append(ev(g.dma_start(T.ATW[64 * e:64 * e + 16, PAD + lo:PAD + hi], T.at[:, R * e + lo:R * e + hi]), 16))

    def bulk(*ks):
        for k, lo, hi in ks:
            if lo >= hi:
                continue
            wait("y", d_c[2 if k < 4 and hi > CX else k // 4])
            ev(SY.dma_start(T.ATW[16 * k:16 * k + 16, PAD + lo:PAD + hi],
                            T.ATW[64 * (k // 4):64 * (k // 4) + 16, PAD + lo:PAD + hi]), 16, d_at if k % 4 > 1 or lo >= x0 else d_a1)

    def repeat(k, lo, hi):
        wait(k, d_a1, *d_c[:2])
        for e in range(2):
            out, in_ = (T.ATW[64 * e + p:64 * e + p + 32, PAD + XP + lo:PAD + XP + hi] for p in (32, 0))
            ev(S.activation(out, in_, AF.Copy) if k == "s" else V.tensor_copy(out, in_) if k == "v" else
               g.affine_select(out, in_, [[0, hi - lo]], A.is_ge, 0.0, 0, 0), 1, r_at)

    def spread(bank, lo, n):
        e = new()
        wait("p", cs["m"], d_cb, d_c[0])
        for x in range(n):
            ev(PE.matmul(bank[:, 128 * x:128 * x + 128], T.Rm[0:32, :],

                         T.ATW[0:32, PAD + lo + 128 * x:PAD + lo + 128 * x + 128], True, True), 1, e)
        return e

    def put(k, e, bank, lo, n):
        wait(k, e)
        out, in_ = T.ATW[:, PAD + lo:PAD + lo + 128 * n], bank[:, 0:128 * n]
        ev(S.activation(out, in_, AF.Copy) if k == "s" else V.tensor_copy(out, in_), 1, r_at)

    if not LATE:
        first(0, 0, CX)
    for k in (PV, PV + 256):
        ev(S.activation(T.pw[:, k:k + 256], T.pw[:, 0:256], AF.Copy), 1, z2)
    wait("s", z0)
    for k in range(PV + 512, PS, 1024):
        n = min(1024, PS - k)
        ev(S.activation(T.pw[:, k:k + n], T.pw[:, 0:n], AF.Copy), 1, z2)
    if PG > PS:
        ev(iota(T.pw[:, PS:PG], [[0, PG - PS]]), 1, z2)

    def consts(names):
        for x in names:
            if x == "1":
                cs[x] = ev(iota(T.X1[:, :], [[2, 8], [16, 16]]))
            if x == "2":
                cs[x] = ev(iota(T.X2[:, :], [[1, 8], [8, 16]]))
            if x == "j":
                cs[x] = ev(iota(T.rowj[:, :], [[4, 2], [128, 16]], 4 * C))
            if x == "i":
                wait("g", m_one)
                cs[x] = select(T.idb[:, :], T.onesb[:, :], [[1, 128]], A.is_equal, 0.0, 0)
            if x == "m":
                cs[x] = select(T.Rm[0:32, :], T.onesb[0:32, :], [[16, 2], [0, 4], [1, 16]], A.is_equal, 0.0, 0)
            if x == "r":
                c_r = select(T.R16[0:16, :], T.onesb[0:16, 0:16], [[8, 2], [1, 2], [2, 4]], A.is_equal, 0.0, 0)
                cs[x] = select(T.rep[0:16, :], T.onesb[0:16, :], [[0, 8], [1, 16]], A.is_equal, 0.0, 0)
                wait("g", c_r)
                c_r = select(T.R16[0:16, 0:4], T.R16[0:16, 0:4], [[2, 4]], A.not_equal, 1.0, 8)
                for lo, w in ((4, 256.0 + PAD), (8, -240.0)):
                    select(T.R16[0:16, lo:lo + 4], T.R16[0:16, lo:lo + 4], [[0, 4]], A.not_equal, w, 15, s=cs[x])
                wait("g", c_r)
                select(T.R16[0:16, 0:4], T.R16[0:16, 0:4], [[0, 4]], A.not_equal, (256.0 + PAD) / 16, 15, s=cs[x])
            if x == "s":
                wait("g", select(T.sele[:, :], T.onesb[:, 0:64], [[16, 2], [1, 16], [32, 2]], A.is_equal, 0.0, 0))
                cs[x] = select(T.sele[:, :], T.sele[:, :], [[16, 2], [1, 16], [32, 2]], A.not_equal, 1.0, 64)

    cs = {}
    consts(GORD[0])

    def keys(r, out, x, e, blocks=range(4)):
        for a in blocks:
            ev(V.tensor_copy(out[32 * a:32 * a + 32, 64 * x:64 * x + 64],
                             T.fkt[32 * r:32 * r + 32, 64 * a:64 * a + 64]), 1, e)
        return e

    k0, k1 = new(), new()
    wait("v", d_lim)
    v_lim = ev(V.tensor_copy(T.limf[0:1, :], T.limi[0:1, :]))
    wait("v", d_fk)
    keys(order[0], T.KS, 0, k0)
    wait("p", v_lim, m_of)
    p_lim = new()
    for e in range(2):
        ev(PE.matmul(T.b3[32 * e:32 * e + 32, 0:2], T.onesf[0:1, :], T.limf[0:1, 2 * e:2 * e + 2], True, True), 1, p_lim)
    wait("v", d_a0, p_lim)
    v_cl = ev(V.tensor_scalar(out=T.b2[0:64, 0:256], in0=T.a0[0:64, :], scalar1=T.b3[0:64, 0:1],
                              scalar2=T.b3[0:64, 1:2], op0=A.max, op1=A.min))
    keys(order[1], T.KS, 1, k1, (0, 1))
    wait("v", v_cl)
    v_ps = ev(V.tensor_tensor(T.ps[0:64, :], T.b2[0:64, 0:256], T.a0[0:64, :], A.is_equal))
    ev(V.memset(T.pw[:, PU:PV], 0.0), 1, z1)
    keys(order[1], T.KS, 1, k1, (2, 3))
    keys(order[2], T.KS, 2, k1)
    wait("v", d_me, c_io)
    v_mp = ev(V.tensor_scalar(out=T.mep[:, 0:32], in0=T.mei[:, :], scalar1=14, scalar2=None, op0=A.arith_shift_right))
    ev(V.tensor_scalar(out=T.mep[:, 32:64], in0=T.mei[:, :], scalar1=0x3F80, scalar2=None, op0=A.bitwise_and), 1, v_mp)
    ev(V.tensor_scalar(out=T.mep[:, 64:96], in0=T.mei[:, :], scalar1=127, scalar2=None, op0=A.bitwise_and), 1, v_mp)
    v_k = new()
    for x, m in enumerate((16, 0x78, 0x6F)):
        ev(V.tensor_scalar(out=T.kb[:, x:x + 1], in0=T.kc[:, :], scalar1=m, scalar2=None, op0=A.bitwise_and), 1, v_k)
    v_kf = ev(V.tensor_copy(T.kf[:, 3:4], T.kc[:, :]))
    v_lo = ev(V.tensor_scalar(out=T.flo[:, :], in0=T.fkt[:, :], scalar1=511, scalar2=None, op0=A.bitwise_and))
    wait("v", v_mp, v_k)
    v_mb = ev(V.tensor_copy(T.meb[:, :], T.mep[:, :]))
    ev(V.tensor_scalar(out=T.kf[:, 0:1], in0=T.kb[:, 0:1], scalar1=15.0 / 256, scalar2=1.0 / 16, op0=A.mult,
                       op1=A.add), 1, v_kf)
    ev(V.tensor_copy(T.kf[:, 1:3], T.kb[:, 1:3]), 1, v_kf)
    kef, pm, pp = (T.kf[:, x:x + 1] for x in (0, 2, 3))
    k_own = keys(q, T.KR, q, new())
    wait("v", v_kf, v_lo)
    v_hi = ev(V.tensor_scalar(out=T.fhib[:, :], in0=T.fkt[:, :], scalar1=BIG - 255.5, scalar2=kef, op0=A.add,
                              op1=A.mult))
    v_lo = ev(V.tensor_scalar(out=T.flob[:, :], in0=T.flo[:, :], scalar1=-256.0, scalar2=kef, op0=A.add, op1=A.mult))
    d_pw = new()
    for a in range(4):
        wait(PWQ[a % 2], v_ps, z1, z2)
        ev(queues[PWQ[a % 2]].dma_start(T.pw[32 * a:32 * a + 32:16, :], T.ps[0:64, :]), 16, d_pw)
    wait("g", k0)
    send(0, "h0_0", T.KS[:, 0:64], T.KR[:, 64 * q:64 * q + 64])
    if LATE:
        first(0, 0, CX)
    consts(GORD[1])
    wait("g", k1)
    send_two("h0_%d", lambda k: T.KS[:, 64 * k:64 * k + 64], T.KR[:, 64 * q:64 * q + 64], "gone")
    consts(GORD[4])
    first(1, 0, R)
    if CX < R:
        first(0, CX, R)
    if BE:
        wait("y", d_pw)
        bulk((1, XP, XP + BE))
    wait("y", "gone")
    bulk((2, x0, x0 + BQ), (3, x0, x0 + B3), (1, XP + BE, B1))
    consts(GORD[2])

    wait("s", m_one)
    s_mel = new()
    for k in range(2):
        ev(S.activation(T.MEL[:, 16 * k:16 * k + 16, 0:8], T.onesb[:, :], AF.Copy, scale=0.0), 1, s_mel)
    ev(S.activation(T.MEL[:, :, 15], T.onesb[:, 0:32], AF.Copy), 1, s_mel)
    ev(S.activation(T.MEL[:, :, 8:16:2], T.onesb[:, :], AF.Copy, scale=-BIG * 17 / 16), 1, s_mel)
    wait("s", v_mb)
    for h in range(2):
        for x in range(3):
            ev(S.activation(T.MEL[:, 16 * h:16 * h + 16, 9 + 2 * x], T.meb[:, 32 * x + h:32 * x + 32:2], AF.Copy,
                            scale=16384.0 if x == 0 else 1.0), 1, s_mel)

    def rows(h):
        wait("p", v_hi, v_lo, c_q, s_mel, cs["i"])
        out = T.b0[:, 256 * h:256 * h + 256]
        PE.matmul(out, T.Qhi[:, 128 * h:128 * h + 128], T.fhib[:, :], True, False)
        for x in range(2):
            PE.matmul(T.b0[:, 256 * h + x:256 * h + 256:2], T.MEL[:, 16 * h + 8 * x:16 * h + 8 * x + 8, :], T.idb[:, :],
                      False, False)
        return PE.matmul(out, T.Qlo[:, 128 * h:128 * h + 128], T.flob[:, :], False, True)

    turn = order + [q]
    CB = [T.b1, T.b2, T.b1, T.b5]
    out_of = []
    wait("v", d_pw, z3)
    wait("s", d_pw, z3)
    wait("p", v_ps)
    done = [new() for n in range(4)]
    c_q = new()

    def evacuate(k):
        wait("v", done[k])
        out = T.CS[:, 32 * k:32 * k + 32]
        out_of.append(ev(V.tensor_scalar(out=out, in0=CB[k][:, 0:32], scalar1=-1.0, scalar2=7.5, op0=A.mult, op1=A.add)
                         if k == 2 else V.tensor_copy(out, CB[k][:, 0:32])))
        wait("g", out_of[k])
        send(k, "h1_%d" % k, T.CS[:, 32 * k:32 * k + 32], T.CR[:, 32 * k:32 * k + 32])

    for n in range(4):
        r = turn[n]
        got = []
        if n == 3:
            for h in range(2):
                for Q, base, col in ((T.Qhi, h - 128.0, pm), (T.Qlo, float(h), pp)):
                    ev(V.tensor_scalar(out=Q[:, 128 * h:128 * h + 128], in0=T.X1[:, :], scalar1=base, scalar2=col,
                                       op0=A.add, op1=A.is_equal), 1, c_q)
            evacuate(2)
            rows(0)
            p_k = ev(rows(1))
        for k, runs in zip("vs", ROUNDS[n]):
            wait(k, "h0_%d" % n if n < 3 else k_own)
            for x, (lo, hi) in enumerate(runs):
                out = T.Pg[:, 1024 * n + 16 * lo:1024 * n + 16 * hi]
                win = T.pw[:, :].indirect(T.KR[:, 64 * r + lo:64 * r + hi])
                got.append((lo, hi, ev(V.tensor_copy(out, win) if k == "v" else S.activation(out, win, AF.Copy))))
                if k == "v" and n in (1, 2) and x == len(runs) - 1:
                    evacuate(n - 1)
                if k == "v" and n == 0:
                    wait("v", cs["1"])
                    wait("p", ev(V.tensor_scalar(out=T.sel4[:, :], in0=T.X1[:, 0:8:2], scalar1=pm, scalar2=None,
                                                 op0=A.is_equal)))
        if n == 2:
            wait("p", out_of[0])
        for u in BLOCKS:
            wait("p", *[e for lo, hi, e in got if lo < 16 * u + 16 and hi > 16 * u])
            for h in range(2):
                i = PE.matmul(CB[n][:, 16 * h + u:16 * h + 16:4],
                              T.Pg[:, 1024 * n + 256 * u + h:1024 * n + 256 * u + 256:2], T.sel4[:, :],
                              n < 3 or (u == BLOCKS[0] and h == 0), n < 3)
                if n < 3:
                    ev(i, 1, done[n])
        if n == 3:
            for k in range(2):
                wait("p", "h1_%d" % k)
                i = PE.matmul(CB[3][:, 0:32], T.idb[:, :], T.CR[:, 32 * k:32 * k + 32], False, k == 1)
            ev(i, 1, done[3])
    g.sem_inc(T.sem.issued, 1)
    total["issued"] = 1
    consts(GORD[3])
    wait("y", done[0], done[1])
    z_w2 = ev(SY.dma_start(T.Pg[0:128:16, 0:C], T.pw[1:128:16, 0:C]), 16)
    if XP:
        wait("y", d_c[1])
        d_cb = ev(SY.dma_start(T.ATW[16:32, PAD:PAD + XP], T.ATW[64:80, PAD:PAD + XP]), 16)
    bulk((5, XP, x0))
    wait("y", "issued")
    bulk((5, x0, R), (1, B1, R), (2, x0 + BQ, R), (3, x0 + B3, R), (6, x0, R), (7, x0, R))
    wait("s", p_k)
    s_k1 = ev(S.activation(T.K1[:, :], T.b0[:, :], AF.Copy))
    wait("v", cs["2"], cs["j"])
    c_m = ev(V.tensor_scalar(out=T.mats[:, 256:384], in0=T.X2[:, :], scalar1=pp, scalar2=None, op0=A.is_equal))
    for x, op in enumerate((A.is_le, A.is_lt)):
        ev(V.tensor_scalar(out=T.mats[:, 128 * x:128 * x + 128], in0=T.X2[:, :], scalar1=pp, scalar2=-1.0, op0=op,
                           op1=A.mult), 1, c_m)
    v_j = new()
    for x, w in enumerate((0.25, -0.25)):
        ev(V.tensor_scalar(out=T.J[:, 32 * x:32 * x + 32], in0=T.rowj[:, :], scalar1=T.kf[:, 1:2], scalar2=w, op0=A.add,
                           op1=A.mult), 1, v_j)
    L1, L1B, IP, ONE = T.mats[:, 0:128], T.mats[:, 128:256], T.mats[:, 256:384], T.onesb[:, :]
    wait("p", c_m, v_j)
    PE.matmul(T.b3[:, 0:32], IP, T.J[:, 0:32], True, False)

    wait("v", done[3], "h1_2")
    v_m = ev(V.tensor_tensor(T.Msk[:, :], CB[3][:, 0:32], T.CR[:, 64:96], A.is_gt))
    wait("v", v_m, v_j)
    v_sc = ev(V.tensor_tensor_scan(T.Sc[:, :], T.Msk[:, 0:16], T.Msk[:, 16:32], 0.0, A.add, A.add))
    v_mj = ev(V.tensor_tensor(T.MJ[:, :], T.Msk[:, :], T.J[:, 32:64], A.mult))
    m_w = ev(V.memset(T.ATW[:, 0:PAD], 0.0))
    wait("p", v_m)
    PE.matmul(T.b3[:, 0:32], L1, T.Msk[:, :], False, False)
    PE.matmul(T.b3[:, 0:16], L1, T.Msk[:, 16:32], False, False)
    PE.matmul(T.b3[:, 16:32], L1B, T.Msk[:, 0:16], False, False)
    wait("p", v_sc)
    PE.matmul(T.b3[:, 0:16], ONE, T.Sc[:, :], False, False)
    PE.matmul(T.b3[:, 16:32], ONE, T.Sc[:, :], False, False)
    wait("p", v_mj)
    p_pos = ev(PE.matmul(T.b3[:, 0:32], IP, T.MJ[:, :], False, True))
    p_nt = ev(PE.matmul(T.b5[:, 256:257], ONE, T.Sc[:, 15:16], True, True))
    if NP[0]:
        p_sp = spread(T.b4, 0, NP[0])
    wait("p", cs["r"], out_of[2])
    p_rl = ev(PE.matmul(T.b1[:, 0:16], T.rep[0:16, :], T.R16[0:16, :], True, True))
    wait("v", p_pos)
    v_o3 = ev(V.tensor_copy(T.off3[:, :], T.b3[:, 0:32]))
    wait("s", p_nt)
    s_nt = ev(S.activation(T.nt[:, :], T.b5[:, 256:257], AF.Copy))
    repeat("s", 0, RS1)
    wait("s", p_rl)
    s_rl = ev(S.activation(T.RL[:, :], T.b1[:, 0:16], AF.Copy))
    s_r1 = ev(S.activation(T.rm3[:, 0:3], T.b1[:, 12:15], AF.Copy, accum_out=T.rm1[:, :]))
    if NP[0]:
        put("s", p_sp, T.b4, 0, NP[0])
    wait("s", s_r1)
    s_rm = ev(S.activation(T.RM[:, :], T.onesb[:, 0:16], AF.Copy, scale=T.rm1[:, :]))
    repeat("s", RS1, RS)
    if RG:
        wait("g", cs["s"], cs["r"])
        repeat("g", RS, RS + RG)

    wait("v", v_o3, s_k1, z_w2)
    v_w1 = ev(V.tensor_copy(T.Pg[:, 0:3584].indirect(T.off3[:, :]), T.K1[:, :]))
    wait("p", v_w1, s_rl, out_of[1])
    p_l = new()
    for c in range(6):
        for j1 in range(2):
            y = 4 * (c // 2) + 2 * j1 + c % 2
            ev(PE.matmul(T.b2[:, y:144:12], T.Pg[:, 768 * j1 + c:768 * j1 + 768:6], T.RL[:, 0:12], True, True), 1, p_l)
    if NP[1]:
        p_sp = spread(T.b7, 128 * NP[0], NP[1])
    wait("s", v_w1)
    wait("v", v_w1)
    s_w2 = [new() for ch in range(3)]
    for c in range(6):
        for jb in range(4):
            out, in_ = T.W2[:, c // 2, :, jb, c % 2, :], T.Pg[:, 384 * jb + c:384 * jb + 384:6]
            ev(V.tensor_copy(out, in_) if 4 * c + jb < WV else S.activation(out, in_, AF.Copy), 1, s_w2[c // 2])
    wait("v", p_l)
    v_z = ev(V.tensor_scalar(out=T.Z[:, :], in0=T.b2[:, 96:144], scalar1=ROUND, scalar2=ROUND, op0=A.add,
                             op1=A.subtract))
    wait("v", v_z)
    v_t = [ev(V.tensor_tensor(T.T2[:, 48 * e:48 * e + 48], T.b2[:, 48 * e:48 * e + 48], T.Z[:, :],
                              A.add if e else A.subtract)) for e in range(2)]
    v_lu = new()
    for e in range(2):
        wait("v", v_t[e])
        for j0 in range(2):
            ev(V.tensor_scalar(out=T.Ls[64 * e:64 * e + 64, :, j0, :], in0=T.T2[64 * j0:64 * j0 + 64, 48 * e:48 * e + 48],
                               scalar1=1.0 if e else 16.0, scalar2=None, op0=A.mult), 1, v_lu)
    wait("g", v_lu)
    for k in range(3):
        send(k, "h2_%d" % k, T.Ls[:, 6 * order[k]:6 * order[k] + 6, :, :], T.Lr[:, 24 * q:24 * q + 24])

    wait("p", s_rm, s_nt)
    for ch in range(3):
        wait("p", s_w2[ch])
        for a in range(4):
            c0 = 64 * ch + 32 * (a % 2) + a // 2
            PE.matmul(T.b5[:, c0:c0 + 31:2], T.W2[:, ch, a, :, :, :], T.RM[:, :], ch + a == 0, False)
    if RV:
        repeat("v", RS + RG, RS + RG + RV)
    if NP[1]:
        put("v", p_sp, T.b7, 128 * NP[0], NP[1])
    wait("v", v_lu)
    v_own = ev(V.tensor_copy(T.Lr[:, 24 * q:24 * q + 24], T.Ls[:, 6 * q:6 * q + 6, :, :]))
    wait("v", d_at, d_a1, r_at, m_w, *d_c)
    wait("s", d_at, d_a1, r_at, m_w, *d_c)
    wait("p", cs["s"], s_k1, s_rl, s_r1, v_o3)

    def gather(k, r, lo, hi):
        out = T.G[:, 384 * r + 16 * lo:384 * r + 16 * hi]
        win = T.ATW[:, :].indirect(T.Lr[:, 24 * r + lo:24 * r + hi])
        return lo, hi, ev(V.tensor_copy(out, win) if k == "v" else S.activation(out, win, AF.Copy))

    def add_up(tile, got, chunks, bank, start=True, stop=True):
        done = new()
        for ch in chunks:
            wait("p", *[e for lo, hi, e in got if lo < 8 * ch + 8 and hi > 8 * ch])
            i = PE.matmul(bank[:, 64 * ch:64 * ch + 64], tile[:, 128 * ch:128 * ch + 128], T.sele[:, :], start,
                          stop and (start or ch == 2))
            if stop and (start or ch == 2):
                ev(i, 1, done)
        return done

    def tile(r):
        return T.G[:, 384 * r:384 * r + 384]

    wait("s", v_own)
    wait("v", v_own)
    if OWNF:
        add_up(tile(q), [gather("v", q, 0, OWNF)] + ([gather("s", q, OWNF, 24)] if OWNF < 24 else []), (2, 0, 1), T.b5,
               False, False)
    got = []
    for k in range(3):
        got.append([])
        for x, runs in zip("vs", SPLIT[k]):
            wait(x, "h2_%d" % k)
            got[k] += [gather(x, order[k], lo, hi) for lo, hi in runs]
    wait("g", *[e for lo, hi, e in got[0]])
    send(0, "h3_0", tile(order[0]), T.L0[:, :])
    if RAW1:
        wait("g", *[e for lo, hi, e in got[1]])
        send(1, "h3_1", tile(order[1]), T.L1[:, :])
        parts = []
    else:
        parts = [(1, add_up(tile(order[1]), got[1], CH[0], T.b1), "h3_1", T.b1, T.S1, T.L1[:, 0:192], 0, 192)]
    if TWO:
        parts += [(2, add_up(tile(order[2]), got[2], (0, 1), T.b0), "h3_2", T.b0, T.S2, T.L2[:, 0:4, :, :], 0, 128),
                  (2, add_up(tile(order[2]), got[2], (2,), T.b2), "h3_3", T.b2, T.S2, T.L2[:, 4:6, :, :], 128, 192)]
    else:
        parts += [(2, add_up(tile(order[2]), got[2], CH[1], T.b0), "h3_2", T.b0, T.S2, T.L2[:, :, :, :], 0, 192)]
    if not OWNF:
        own = [gather("s", q, 8 * x, 8 * x + 8) for x in range(3)]
    for k, p, rsem, bank, out, dst, lo, hi in parts:
        wait("v", p)
        wait("g", ev(V.transpose(out[:, lo:hi], bank[:, lo:hi])))
        send(k, rsem, out[:, lo:hi], dst)
    if not OWNF:
        add_up(tile(q), own, range(3), T.b5, False, False)
    wait("p", "h3_0")
    a = add_up(T.L0, [], range(3), T.b5, False, not RAW1)
    if RAW1:
        wait("p", "h3_1")
        a = add_up(T.L1, [], range(3), T.b5, False, True)
    wait("g", s_nt)
    ev(g.dma_start(T.y[:, C:C + 1], T.nt[0:16, :], allow_slow_non_contiguous=True), 16)

    wait("v", a)
    a = ev(V.transpose(T.bT[:, 0:6, :, :], T.b5[:, 0:192]))
    if not RAW1:
        wait("v", a, "h3_1")
        a = ev(V.tensor_tensor(T.bT[:, 0:6, :, :], T.bT[:, 0:6, :, :], T.L1[:, 0:192], A.add))
    x = new()
    for c in range(6):
        ch, xl = c // 2, c % 2
        wait("v", a, "h3_3" if ch == 2 and TWO else "h3_2")
        ev(V.tensor_tensor(T.O[:, c:192:6], T.bT[:, 2 * ch:2 * ch + 2, xl, :], T.L2[:, 2 * ch:2 * ch + 2, xl, :], A.add),
           1, x)
    for n, jbs in (("y", (0, 1)), ("s", (2, 3))):
        wait(n, x)
        for jb in jbs:
            ev(queues[n].dma_start(T.y[:, 384 * jb:384 * jb + 384], T.O[32 * jb:32 * jb + 32, :]), 16)

    for s in total:
        if waited.get(s, 0) < total[s]:
            wait("g", s)
